import numpy as np, ml_dtypes
CORES = [3,7,11,15,131,135,139,143]
N = 8
import mx_ref
BF = ml_dtypes.bfloat16
def cols(t, e):
    v = np.concatenate([t.reshape(128, -1, 4), np.zeros((128, 1, 4), BF)], axis=1)
    return np.ascontiguousarray(v[:, e]).reshape(128, -1)
def decode(q):
    o = []
    for b in range(4):
        e = np.zeros((128, 128, 4), np.float32); e[np.arange(128), np.arange(128), b] = 1
        o.append(mx_ref.matmul(mx_ref.quantize(e.reshape(128, 512).astype(BF)), q))
    return np.stack(o, axis=2).reshape(128, -1)
def f(rng, *shape):
    return mx_ref.flush((rng.standard_normal(shape, dtype=np.float32) * np.exp2(rng.integers(-2, 3, shape[:-1] + (1,)))).astype(BF))
def wide(rng, *shape, cols=0):
    v = rng.standard_normal(shape, dtype=np.float32) * np.exp2(rng.integers(-12, 13, shape)).astype(np.float32)
    if cols: v *= np.repeat(np.exp2(rng.integers(-cols, cols + 1, shape[:-2] + (1, shape[-1] // 4))) * (rng.random(shape[:-2] + (1, shape[-1] // 4)) > 0.0625), 4, axis=-1).astype(np.float32)
    return mx_ref.flush(v.astype(BF))
T, K = 256, 32
def setup_inputs(rng):
    u = np.zeros((N, 128, 512), BF); u[:, :, :4] = f(rng, N, 128, 4)
    return {"gr": f(rng, N, 128, 4 * T), "u": u}
def raised(rng, chosen):
    d = setup_inputs(rng)
    for r in range(N):
        g = d["gr"][r].astype(np.float32).reshape(128, T, 4)
        sign = np.where(d["u"][r][:, :4].astype(np.float32) < 0, -1, 1).reshape(128, 1, 4) * rng.choice([-1, 1], K).reshape(1, K, 1)
        v = g * np.float32(2.0 ** -8)
        v[:, chosen[r]] = np.abs(g[:, chosen[r]]) * sign
        d["gr"][r] = mx_ref.flush(v.reshape(128, 4 * T).astype(BF))
    return d
def setup_inputs_same(rng):
    d = raised(rng, [rng.permutation(T)[:K]] * N)
    k = rng.permutation(np.concatenate([[12, -12, -11], rng.integers(-12, 13, N - 3)]))
    d["gr"] = mx_ref.flush((d["gr"].astype(np.float32) * np.exp2(k).astype(np.float32).reshape(N, 1, 1)).astype(BF))
    return d
def setup_inputs_apart(rng):
    p = rng.permutation(T)
    return raised(rng, [p[(r * K + np.arange(K)) % T] for r in range(N)])
def setup_inputs_ties(rng):
    d = setup_inputs(rng); n = T // 11
    for r in range(N):
        p = rng.permutation(T)[:11 * n]
        e = np.full(T, -1); e[p] = np.repeat(np.arange(n), 11)
        s = rng.choice([-1, 1], (n, 11)); s[:, 0] = 1; s[:, 1] = -1
        sign = np.ones(T, np.float32); sign[p] = s.reshape(-1)
        d["gr"][r] = (cols(d["gr"][r], e).astype(np.float32).reshape(128, T, 4) * sign.reshape(1, T, 1)).reshape(128, 4 * T).astype(BF)
    return d
def setup_inputs_few(rng):
    d = setup_inputs(rng); p = rng.permutation(N)
    d["u"][p[0]] = 0
    sign = rng.choice([-1, 1], (128, 1, 4))
    d["u"][p[1]][:, :4] = (sign * rng.uniform(1, 4, (128, 1, 4)) * 2.0 ** 28).reshape(128, 4).astype(BF)
    d["gr"][p[1]] = (sign * rng.choice([-1, 1], (1, T, 1)) * rng.uniform(1, 4, (128, T, 4)) * 2.0 ** 28).reshape(128, 4 * T).astype(BF)
    for r in p[2:2 + N // 2]:
        k = rng.permutation(T)[:rng.integers(1, K)]
        e = np.full(T, -1); e[k] = k
        d["gr"][r] = cols(d["gr"][r], e)
    return d
def setup_inputs_spread(rng):
    d = setup_inputs(rng); d["gr"] = wide(rng, N, 128, 4 * T, cols=8); return d
def check_inputs(d):
    return ["u"] if (d["u"][:, :, 4:].astype(np.float32) != 0).any() else []
def reference(gr, u):
    acc = np.zeros((128, T, 4), np.float32); nb = np.zeros((N, K), np.float32); sc = np.zeros((N, 1, K), np.float32)
    er = gr.astype(np.float32).reshape(N, 128, T, 4)
    for s in range(N):
        score = np.abs(mx_ref.matmul(mx_ref.quantize(u[s]), mx_ref.quantize(gr[s]))[0]) + np.float32(0.0)
        e = np.argsort(-score, kind="stable")[:K]
        v = decode(mx_ref.quantize(cols(gr[s], e))).reshape(128, K, 4)
        acc[:, e] = acc[:, e] + v
        er[s][:, e] = er[s][:, e] - v
        nb[s] = e
        sc[s, 0] = score[e]
    return {"acc": np.stack([acc.reshape(128, 4 * T)] * N), "er": er.reshape(N, 128, 4 * T), "nb": np.stack([nb] * N), "sc": sc}

@@ -1,0 +1,305 @@
+from concourse.bass import DstId, RemoteDMATransfer
+from concourse.mybir import dt, AluOpType, AxisListType, ActivationFunctionType
+
+K = 32
+TINY = 2.0 ** -120
+PRED = 1.0 - 2.0 ** -24
+
+F, B, I, U = "float32", "bfloat16", "int32", "uint16"
+C8, S8 = "float8_e4m3fn_x4", "uint8"
+SCRATCH = {
+    "grb": ("sbuf", [128, 1024], B), "urep": ("sbuf", [128, 512], B), "hb": ("sbuf", [128, 512], B),
+    "eb": ("sbuf", [128, 528], B),
+    "gq": ("sbuf", [128, 256], C8), "gs": ("sbuf", [128, 256], S8),
+    "uq": ("sbuf", [128, 128], C8), "us": ("sbuf", [128, 128], S8),
+    "eq": ("sbuf", [128, 512], C8), "es": ("sbuf", [128, 512], S8),
+    "qb": ("sbuf", [128, 160], C8), "qs": ("sbuf", [128, 160], S8),
+    "cb": ("sbuf", [128, 192], C8), "cs": ("sbuf", [128, 192], S8),
+    "lp": ("sbuf", [128, 16], U), "ll": ("sbuf", [128, 24], U),
+    "li": ("sbuf", [128, 32], I), "l8": ("sbuf", [128, 64], I), "off": ("sbuf", [128, 64], U), "ofo": ("sbuf", [128, 8], U),
+    "ab": ("sbuf", [128, 256], F), "ad": ("sbuf", [128, 256], F), "wt": ("sbuf", [128, 256], F),
+    "sraw": ("sbuf", [128, 8], F), "sth": ("sbuf", [128, 8], F),
+    "cmp": ("sbuf", [128, 512], B), "rks": ("sbuf", [128, 256], B), "rkf": ("sbuf", [128, 8], F),
+    "i32": ("sbuf", [128, 32], F), "coln": ("sbuf", [128, 2], B), "pi": ("sbuf", [128, 8], I), "p4": ("sbuf", [128, 8], F),
+    "ai": ("sbuf", [128, 32], F), "mk": ("sbuf", [128, 32], F), "r4": ("sbuf", [128, 32], F), "r8": ("sbuf", [128, 32], F),
+    "vv": ("sbuf", [128, 64], F), "vt": ("sbuf", [128, 64], F), "q4": ("sbuf", [128, 8], F), "rc": ("sbuf", [128, 8], F),
+    "xx": ("sbuf", [128, 32], F), "xt": ("sbuf", [128, 32], F), "sg4": ("sbuf", [128, 32], F), "sg8": ("sbuf", [128, 32], F),
+    "wv": ("sbuf", [128, 64], F), "wt2": ("sbuf", [128, 64], F), "wq": ("sbuf", [128, 8], F), "wx": ("sbuf", [128, 32], F),
+    "wy": ("sbuf", [128, 32], F),
+    "lf": ("sbuf", [128, 64], F), "nt": ("sbuf", [128, 64], F), "nc": ("sbuf", [128, 8], F),
+    "acb": ("sbuf", [128, 1024], F), "erb": ("sbuf", [128, 1024], F), "vb": ("sbuf", [128, 1024], F),
+    "tm": ("sbuf", [128, 128], F), "te": ("sbuf", [128, 128], F),
+    "pa": ("psum", [128, 2048], F), "pb": ("psum", [128, 2048], F),
+}
+SEMAPHORES = ["v", "s", "t", "p", "dgr", "du", "dsc", "dnb", "der", "dac", "l1", "c1", "s1", "l2", "c2", "s2", "sent"]
+
+
+def rank_program(g, core, T, topo):
+    rank = T.rank_of(core)
+    if rank is None:
+        return
+    V, S, P, Y = g.vector, g.scalar, g.tensor, g.sync
+    Q = {"v": V, "s": S, "t": P, "p": g, "y": Y}
+    A, AF, X = AluOpType, ActivationFunctionType, AxisListType.X
+    cnt, seen = {"sent": 0}, {}
+
+    def done(sem, ins, n=1):
+        ins.then_inc(T.sem[sem], n)
+        cnt[sem] = cnt.get(sem, 0) + n
+        return (sem, cnt[sem])
+
+    def need(queue, *toks):
+        for sem, n in toks:
+            if seen.get((queue, sem), 0) < n:
+                Q[queue].wait_ge(T.sem[sem], n)
+                seen[(queue, sem)] = n
+
+    partner = [c for c in T.cores if c != core and c in topo.cores_of(core)][0]
+    peers = [c for c in T.cores if c not in topo.cores_of(core) and topo.die(c) == topo.die(core)]
+    first = rank < T.rank_of(partner)
+
+    def pair(c):
+        return min(T.rank_of(d) for d in T.cores if d in topo.cores_of(c)) // 2
+
+    me = pair(core)
+
+    def slot(src, dst):
+        return pair(src) - (1 if pair(src) > pair(dst) else 0)
+
+    m2 = topo.mask(core, peers[0])
+    for c in peers:
+        m2 &= topo.mask(core, c)
+    m1 = m2 & topo.mask(core, partner)
+    n1, n2 = bin(m1).count("1"), bin(m2).count("1")
+    q0 = 0 if first else 32
+    own0 = 96 if first else 32
+    pair0 = 96 if first else 0
+    dec0 = 32 if first else 0
+    lown = 4 if first else 8
+    far_c, far_l = (0, 4) if first else (128, 8)
+
+    d_u = done("du", S.dma_start(T.urep[:, 0:4], T.u[:, 0:4]), 16)
+    d_g = done("dgr", Y.dma_start(T.grb[:], T.gr[:]), 16)
+
+    k_eb = done("v", V.memset(T.eb[:], 1.0))
+    k_wt = done("v", V.memset(T.wt[:], 1.0))
+    done("p", g.iota(T.i32[:], [[1, 32]], 0, 0, allow_small_or_imprecise_dtypes=True))
+    done("p", g.iota(T.coln[:], [[128, 2]], 0, 1, allow_small_or_imprecise_dtypes=True))
+    done("p", g.iota(T.ai[:], [[0, 2], [1, 4], [0, 4]], 0, 0, allow_small_or_imprecise_dtypes=True))
+    k_p = done("p", g.iota(T.pi[:, 0:1], [[1, 1]], 0, 1))
+    need("p", k_wt)
+    k_wt = done("p", g.affine_select(T.wt[:], T.wt[:], [[0, 2], [-1, 128]], A.is_gt, PRED, 0, 1))
+    need("p", k_eb)
+    k_eb = done("p", g.affine_select(T.eb[:, 0:516], T.eb[:, 0:516], [[-1, 516]], A.is_equal, 0.0, 3, 4))
+    done("v", V.memset(T.hb[:], 0.0))
+    done("v", V.memset(T.r4[:], 1.0))
+    k = done("v", V.memset(T.r8[:], 1.0))
+    done("v", V.memset(T.wx[:], 0.0))
+    need("v", k)
+    done("v", V.memset(T.r4[:, 0:32:4], 0.0))
+    done("v", V.memset(T.r8[:, 0:32:8], 0.0))
+    done("v", V.memset(T.r8[:, 4:32:8], 256.0))
+    need("v", k_p)
+    k = done("v", V.tensor_scalar(T.pi[:, 1:2], T.pi[:, 0:1], 3, None, A.bitwise_and))
+    need("v", k)
+    k = done("v", V.tensor_copy(T.p4[:, 0:1], T.pi[:, 1:2]))
+    need("v", k)
+    done("v", V.tensor_scalar(T.mk[:], T.ai[:], T.p4[:, 0:1], None, A.is_equal))
+
+    need("v", d_u)
+    w = 4
+    while w < 512:
+        k = done("v", V.tensor_copy(T.urep[:, w:2 * w], T.urep[:, 0:w]))
+        need("v", k)
+        w *= 2
+    k_u = done("v", V.quantize_mx(T.uq[:], T.us[:], T.urep[:]))
+    need("v", d_g)
+    k_g = done("v", V.quantize_mx(T.gq[:], T.gs[:], T.grb[:]))
+
+    need("t", k_u, k_g)
+    t_f = done("t", P.matmul_mx(T.pa[:, 0:256], T.uq[:], T.us[:], T.gq[:], T.gs[:], True, True))
+    t_0 = done("t", P.matmul_mx(T.pa[:, 512:640], T.gq[:, 0:128], T.gs[:, 0:128], T.uq[:], T.us[:], True, True))
+    t_1 = done("t", P.matmul_mx(T.pa[:, 1024:1152], T.gq[:, 128:256], T.gs[:, 128:256], T.uq[:], T.us[:], True, True))
+    need("s", t_f)
+    a_f = done("s", S.activation(T.ab[:], T.pa[:, 0:256], AF.Abs, bias=TINY))
+    need("v", t_0)
+    done("v", V.tensor_reduce(T.sraw[:, 0:1], T.pa[:, 512:513], X, A.max, apply_absolute_value=True))
+    need("v", t_1)
+    k = done("v", V.tensor_reduce(T.sraw[:, 1:2], T.pa[:, 1024:1025], X, A.max, apply_absolute_value=True))
+    need("v", k)
+    k_th = done("v", V.tensor_scalar(T.sth[:, 0:2], T.sraw[:, 0:2], TINY, None, A.max))
+
+    need("v", a_f, k_wt)
+    k_d = done("v", V.tensor_tensor(T.ad[:], T.ab[:], T.wt[:], A.mult))
+    need("v", k_th)
+    s0, s1 = T.sth[:, 0:1], T.sth[:, 1:2]
+    done("v", V.tensor_scalar(T.cmp[:, 128:256], T.ab[:, 128:256], s0, None, A.is_gt))
+    done("v", V.tensor_scalar(T.cmp[:, 256:384], T.ab[:, 0:128], s1, None, A.is_ge))
+    need("v", k_d)
+    k0 = done("v", V.tensor_scalar(T.cmp[:, 0:128], T.ad[:, 0:128], s0, None, A.is_ge))
+    k1 = done("v", V.tensor_scalar(T.cmp[:, 384:512], T.ad[:, 128:256], s1, None, A.is_ge))
+    need("v", k0)
+    k0 = done("v", V.tensor_tensor_scan(T.rks[:, 0:128], T.cmp[:, 0:128], T.cmp[:, 128:256], 0.0, A.add, A.add))
+    need("v", k1)
+    k1 = done("v", V.tensor_tensor_scan(T.rks[:, 128:256], T.cmp[:, 256:384], T.cmp[:, 384:512], 0.0, A.add, A.add))
+    rk = [T.rks[:, 127:128], T.rks[:, 255:256]]
+
+    need("v", k_p, k0)
+    done("v", V.tensor_scalar(T.vv[:, 0:32], T.i32[:], rk[0], T.coln[:, 0:1], A.is_equal, A.mult))
+    need("v", k1)
+    k = done("v", V.tensor_scalar(T.vv[:, 32:64], T.i32[:], rk[1], T.coln[:, 1:2], A.is_equal, A.mult))
+    need("v", k)
+    k = done("v", V.transpose(T.vt[:], T.vv[:]))
+    need("v", k)
+    for a in range(4):
+        k = done("v", V.tensor_reduce(T.q4[0:32, a:a + 1], T.vt[32 * a:32 * a + 32, :], X, A.add))
+    need("v", k)
+    k = done("v", V.tensor_reduce(T.rc[0:32, 0:1], T.q4[0:32, 0:4], X, A.add))
+    need("v", k)
+    for a in range(4):
+        k = done("v", V.tensor_scalar(T.xx[32 * a:32 * a + 32, :], T.mk[0:32, :], T.rc[0:32, 0:1], None, A.mult))
+    need("v", k)
+    k = done("v", V.transpose(T.xt[:], T.xx[:]))
+    need("v", k)
+    k4 = done("v", V.tensor_tensor_scan(T.sg4[:], T.r4[:], T.xt[:], 0.0, A.mult, A.add))
+    k8 = done("v", V.tensor_tensor_scan(T.sg8[:], T.r8[:], T.xt[:], 0.0, A.mult, A.add))
+    need("v", k4)
+    k_o = done("v", V.tensor_scalar(T.ofo[:], T.sg4[:, 3:32:4], 4.0, T.p4[:, 0:1], A.mult, A.add))
+    need("v", k8)
+    k_lp = done("v", V.tensor_copy(T.lp[:, lown:lown + 4], T.sg8[:, 7:32:8]))
+    need("v", k_o)
+    h0 = 4 * (own0 - q0)
+    k = done("v", V.tensor_copy(T.hb[:, h0:h0 + 128], T.grb[:, 0:1024].indirect(T.ofo[:, 0:8])))
+    need("v", k)
+    k_q = done("v", V.quantize_mx(T.qb[:, q0:q0 + 128], T.qs[:, q0:q0 + 128], T.hb[:]))
+
+    rid, pid = topo.addr(partner, core)
+    b8 = dt.uint8
+
+    def hop1(out, in_, sem):
+        g.remote_dma(out_ap=out, in_ap=in_, remote_sem=T.sem[sem], local_sem=T.sem.sent, pid=pid, routing_id=rid, dma_engine_mask=m1)
+        cnt["sent"] += n1
+
+    def hop2(dst, src, sem):
+        ids, outs = [], []
+        for c in peers:
+            r_, p_ = topo.addr(c, core)
+            ids.append(DstId(rid=r_, pnc=p_))
+            outs.append(dst(slot(core, c)))
+        g.remote_dma_fused([RemoteDMATransfer(dst_ids=ids, dma_engine_mask=m2, remote_sem=T.sem[sem], srcs=[src], dsts=outs)], local_sem=T.sem.sent)
+        cnt["sent"] += n2
+
+    L1, C1, S1 = ("l1", n1), ("c1", n1), ("s1", n1)
+    L2, C2, S2 = ("l2", 3 * n2), ("c2", 3 * n2), ("s2", 3 * n2)
+    need("p", k_lp)
+    hop1(T.lp[:, far_l:far_l + 4], T.lp[:, lown:lown + 4], "l1")
+    need("p", k_q)
+    hop1(T.qb[:, far_c:far_c + 32].bitcast(b8), T.qb[:, own0:own0 + 32].bitcast(b8), "c1")
+    hop1(T.qs[:, far_c:far_c + 32], T.qs[:, own0:own0 + 32], "s1")
+    need("p", L1)
+    hop2(lambda i: T.ll[:, 8 * i:8 * i + 8], T.lp[:, 4:12], "l2")
+    need("p", C1)
+    hop2(lambda i: T.cb[:, 64 * i:64 * i + 64].bitcast(b8), T.qb[:, pair0:pair0 + 64].bitcast(b8), "c2")
+    need("p", S1)
+    hop2(lambda i: T.cs[:, 64 * i:64 * i + 64], T.qs[:, pair0:pair0 + 64], "s2")
+
+    need("s", d_g)
+    a_e = done("s", S.activation(T.erb[:], T.grb[:], AF.Copy))
+    need("v", k_eb)
+    for b in range(4):
+        k_e = done("v", V.quantize_mx(T.eq[:, 128 * b:128 * b + 128], T.es[:, 128 * b:128 * b + 128], T.eb[:, 3 - b:515 - b]))
+    done("v", V.tensor_copy(T.rkf[:, 0:1], rk[0]))
+    k = done("v", V.tensor_copy(T.rkf[:, 1:2], rk[1]))
+    k_z = done("v", V.memset(T.acb[:], 0.0))
+    need("v", k)
+    for h in range(2):
+        k = done("v", V.tensor_scalar(T.wv[:, 32 * h:32 * h + 32], T.i32[:], T.rkf[:, h:h + 1], T.sraw[:, h:h + 1], A.is_equal, A.mult))
+    need("v", k)
+    k = done("v", V.transpose(T.wt2[:], T.wv[:]))
+    need("v", k)
+    for a in range(4):
+        k = done("v", V.tensor_reduce(T.wq[0:32, a:a + 1], T.wt2[32 * a:32 * a + 32, :], X, A.add))
+    need("v", k)
+    k = done("v", V.tensor_reduce(T.wx[0:32, 0:1], T.wq[0:32, 0:4], X, A.add))
+    need("v", k)
+    k_sc = done("v", V.transpose(T.wy[0:32, :], T.wx[0:32, :]))
+    need("y", k_sc)
+    d_sc = done("dsc", Y.dma_start(T.sc[:], T.wy[0:1, :]), 16)
+
+    def decode(ps, n, codes, scales):
+        return [done("t", P.matmul_mx(ps[:, 512 * b:512 * b + n], T.eq[:, 128 * b:128 * b + 128], T.es[:, 128 * b:128 * b + 128],
+                                      codes, scales, True, True)) for b in range(4)]
+
+    need("t", k_e, a_f, k_th, C1, S1)
+    td = decode(T.pa, 128, T.qb[:, dec0:dec0 + 128], T.qs[:, dec0:dec0 + 128])
+    c0 = pair0 - dec0
+    va = []
+    for b in range(4):
+        src, dst = T.pa[:, 512 * b + c0:512 * b + c0 + 64], T.vb[:, b:256:4]
+        if b % 2:
+            need("s", td[b])
+            va.append(done("s", S.activation(dst, src, AF.Copy)))
+        else:
+            need("v", td[b])
+            va.append(done("v", V.tensor_copy(dst, src)))
+    o = 0 if first else 128
+    need("v", a_e, *va)
+    k = done("v", V.tensor_tensor(T.te[:], T.erb[:, 0:1024].indirect(T.ofo[:, 0:8]), T.vb[:, o:o + 128], A.subtract))
+    need("v", k)
+    k_er = done("v", V.tensor_copy(T.erb[:, 0:1024].indirect(T.ofo[:, 0:8]), T.te[:]))
+    need("y", k_er)
+    d_er = done("der", Y.dma_start(T.er[:], T.erb[:]), 16)
+
+    need("v", L1, k_lp)
+    k = done("v", V.tensor_copy(T.li[:, 8 * me:8 * me + 8], T.lp[:, 4:12]))
+    need("v", L2)
+    if me > 0:
+        k = done("v", V.tensor_copy(T.li[:, 0:8 * me], T.ll[:, 0:8 * me]))
+    if me < 3:
+        k = done("v", V.tensor_copy(T.li[:, 8 * me + 8:32], T.ll[:, 8 * me:24]))
+    need("v", k)
+    done("v", V.tensor_scalar(T.l8[:, 0:64:2], T.li[:], 8, None, A.logical_shift_right))
+    k = done("v", V.tensor_scalar(T.l8[:, 1:64:2], T.li[:], 255, None, A.bitwise_and))
+    need("v", k)
+    k_of = done("v", V.tensor_scalar(T.off[:], T.l8[:], 4.0, T.p4[:, 0:1], A.mult, A.add))
+    k = done("v", V.tensor_copy(T.lf[0:32, :], T.l8[0:32, :]))
+    need("v", k)
+    k = done("v", V.transpose(T.nt[0:32, :], T.lf[0:32, :]))
+    need("v", k)
+    done("v", V.tensor_copy(T.nc[0:32, 0:4], T.nt[0:32, 0:16:4]))
+    k_nb = done("v", V.tensor_copy(T.nc[0:32, 4:8], T.nt[0:32, 32:48:4]))
+    need("y", k_nb)
+    done("dnb", Y.dma_start(T.nb[0:4, :], T.nc[0:32, 0:4]), 16)
+    d_nb = done("dnb", Y.dma_start(T.nb[4:8, :], T.nc[0:32, 4:8]), 16)
+
+    need("t", C2, S2)
+    td = decode(T.pb, 192, T.cb[:], T.cs[:])
+    vl = []
+    for b in (1, 3):
+        need("s", td[b])
+        vl.append(done("s", S.activation(T.vb[:, 256 + b:1024:4], T.pb[:, 512 * b:512 * b + 192], AF.Copy)))
+
+    need("v", k_of, k_z)
+    emptied = False
+    for s in range(8):
+        m = s // 2
+        if m != me and not emptied:
+            emptied = True
+            for b in (0, 2):
+                need("v", td[b])
+                vl.append(done("v", V.tensor_copy(T.vb[:, 256 + b:1024:4], T.pb[:, 512 * b:512 * b + 192])))
+            need("v", *vl)
+        at = (s % 2) if m == me else 2 + 2 * (m - (1 if m > me else 0)) + s % 2
+        v = T.vb[:, 128 * at:128 * at + 128]
+        win = T.acb[:, 0:1024].indirect(T.off[:, 8 * s:8 * s + 8])
+        if s:
+            need("v", k)
+            k = done("v", V.tensor_tensor(T.tm[:], win, v, A.add))
+            need("v", k)
+            v = T.tm[:]
+        k = done("v", V.tensor_copy(win, v))
+    need("y", k)
+    d_ac = done("dac", Y.dma_start(T.acc[:], T.acb[:]), 16)
+
+    need("p", d_u, d_g, d_sc, d_er, d_nb, d_ac, L2, C2, S2)
+    need("p", *[(x, cnt[x]) for x in ("v", "s", "t", "p", "sent")])

@@ -4,34 +4,40 @@ from concourse.mybir import dt, AluOpType, AxisListType, ActivationFunctionType
 K = 32
 TINY = 2.0 ** -120
 PRED = 1.0 - 2.0 ** -24
+HOLD = 2.0 ** 40
 
 F, B, I, U = "float32", "bfloat16", "int32", "uint16"
 C8, S8 = "float8_e4m3fn_x4", "uint8"
 SCRATCH = {
-    "grb": ("sbuf", [128, 1024], B), "urep": ("sbuf", [128, 512], B), "hb": ("sbuf", [128, 512], B),
-    "eb": ("sbuf", [128, 528], B),
+    "grb": ("sbuf", [128, 1024], B), "ub": ("sbuf", [128, 16], B), "urep": ("sbuf", [128, 512], B), "hb": ("sbuf", [128, 512], B),
+    "eb": ("sbuf", [128, 528], B), "uo": ("sbuf", [128, 16], U),
     "gq": ("sbuf", [128, 256], C8), "gs": ("sbuf", [128, 256], S8),
     "uq": ("sbuf", [128, 128], C8), "us": ("sbuf", [128, 128], S8),
     "eq": ("sbuf", [128, 512], C8), "es": ("sbuf", [128, 512], S8),
     "qb": ("sbuf", [128, 160], C8), "qs": ("sbuf", [128, 160], S8),
     "cb": ("sbuf", [128, 192], C8), "cs": ("sbuf", [128, 192], S8),
-    "lp": ("sbuf", [128, 16], U), "ll": ("sbuf", [128, 24], U),
-    "li": ("sbuf", [128, 32], I), "l8": ("sbuf", [128, 64], I), "off": ("sbuf", [128, 64], U), "ofo": ("sbuf", [128, 8], U),
-    "ab": ("sbuf", [128, 256], F), "ad": ("sbuf", [128, 256], F), "wt": ("sbuf", [128, 256], F),
-    "sraw": ("sbuf", [128, 8], F), "sth": ("sbuf", [128, 8], F),
+    "lp": ("sbuf", [128, 16], U), "ll": ("sbuf", [128, 16], U), "ofo": ("sbuf", [128, 8], U),
+    "offp": ("sbuf", [128, 56], U), "offl": ("sbuf", [128, 64], U),
+    "ab": ("sbuf", [128, 256], F), "th": ("sbuf", [128, 256], F), "wt": ("sbuf", [128, 128], F),
+    "sth": ("sbuf", [128, 8], F),
     "cmp": ("sbuf", [128, 512], B), "rks": ("sbuf", [128, 256], B), "rkf": ("sbuf", [128, 8], F),
-    "i32": ("sbuf", [128, 32], F), "coln": ("sbuf", [128, 2], B), "pi": ("sbuf", [128, 8], I), "p4": ("sbuf", [128, 8], F),
-    "ai": ("sbuf", [128, 32], F), "mk": ("sbuf", [128, 32], F), "r4": ("sbuf", [128, 32], F), "r8": ("sbuf", [128, 32], F),
+    "i32": ("sbuf", [128, 32], F), "coln": ("sbuf", [128, 2], B), "pi": ("sbuf", [128, 8], I), "pf": ("sbuf", [128, 8], F),
+    "ai": ("sbuf", [128, 32], F), "bi": ("sbuf", [128, 32], F), "kk": ("sbuf", [128, 32], F),
+    "mk": ("sbuf", [128, 64], F), "r4": ("sbuf", [128, 32], F), "r16": ("sbuf", [128, 32], F),
+    "ce": ("sbuf", [128, 32], F), "cg": ("sbuf", [128, 32], F), "ch": ("sbuf", [128, 256], B),
     "vv": ("sbuf", [128, 64], F), "vt": ("sbuf", [128, 64], F), "q4": ("sbuf", [128, 8], F), "rc": ("sbuf", [128, 8], F),
-    "xx": ("sbuf", [128, 32], F), "xt": ("sbuf", [128, 32], F), "sg4": ("sbuf", [128, 32], F), "sg8": ("sbuf", [128, 32], F),
+    "xx": ("sbuf", [128, 64], F), "xt": ("sbuf", [128, 64], F), "sg4": ("sbuf", [128, 32], F), "sg16": ("sbuf", [128, 32], F),
     "wv": ("sbuf", [128, 64], F), "wt2": ("sbuf", [128, 64], F), "wq": ("sbuf", [128, 8], F), "wx": ("sbuf", [128, 32], F),
-    "wy": ("sbuf", [128, 32], F),
-    "lf": ("sbuf", [128, 64], F), "nt": ("sbuf", [128, 64], F), "nc": ("sbuf", [128, 8], F),
+    "wy": ("sbuf", [128, 32], F), "zz": ("sbuf", [128, 16], F),
+    "lf": ("sbuf", [128, 32], F), "nt": ("sbuf", [128, 32], F),
+    "ent": ("sbuf", [128, 256], B), "lm": ("sbuf", [128, 256], B), "pr": ("sbuf", [128, 256], B),
+    "hp": ("sbuf", [128, 256], B), "hl": ("sbuf", [128, 256], B),
+    "tv": ("sbuf", [128, 1032], F),
     "acb": ("sbuf", [128, 1024], F), "erb": ("sbuf", [128, 1024], F), "vb": ("sbuf", [128, 1024], F),
-    "tm": ("sbuf", [128, 128], F), "te": ("sbuf", [128, 128], F),
+    "vo": ("sbuf", [128, 128], F), "te": ("sbuf", [128, 128], F),
     "pa": ("psum", [128, 2048], F), "pb": ("psum", [128, 2048], F),
 }
-SEMAPHORES = ["v", "s", "t", "p", "dgr", "du", "dsc", "dnb", "der", "dac", "l1", "c1", "s1", "l2", "c2", "s2", "sent"]
+SEMAPHORES = ["v", "s", "t", "p", "dgr", "du", "dsc", "dnb", "der", "dac", "l1", "c1", "s1", "c2", "s2", "sent", "left"]
 
 
 def rank_program(g, core, T, topo):
@@ -41,7 +47,7 @@ def rank_program(g, core, T, topo):
     V, S, P, Y = g.vector, g.scalar, g.tensor, g.sync
     Q = {"v": V, "s": S, "t": P, "p": g, "y": Y}
     A, AF, X = AluOpType, ActivationFunctionType, AxisListType.X
-    cnt, seen = {"sent": 0}, {}
+    cnt, seen = {"sent": 0, "left": 0}, {}
 
     def done(sem, ins, n=1):
         ins.then_inc(T.sem[sem], n)
@@ -56,6 +62,7 @@ def rank_program(g, core, T, topo):
 
     partner = [c for c in T.cores if c != core and c in topo.cores_of(core)][0]
     peers = [c for c in T.cores if c not in topo.cores_of(core) and topo.die(c) == topo.die(core)]
+    others = [c for c in T.cores if c not in topo.cores_of(core)]
     first = rank < T.rank_of(partner)
 
     def pair(c):
@@ -64,87 +71,101 @@ def rank_program(g, core, T, topo):
     me = pair(core)
 
     def slot(src, dst):
-        return pair(src) - (1 if pair(src) > pair(dst) else 0)
+        return src - (1 if src > dst else 0)
 
-    m2 = topo.mask(core, peers[0])
-    for c in peers:
+    m2 = topo.mask(core, others[0])
+    for c in others:
         m2 &= topo.mask(core, c)
-    m1 = m2 & topo.mask(core, partner)
+    m1 = topo.mask(core, partner) & ~m2
     n1, n2 = bin(m1).count("1"), bin(m2).count("1")
     q0 = 0 if first else 32
     own0 = 96 if first else 32
     pair0 = 96 if first else 0
     dec0 = 32 if first else 0
-    lown = 4 if first else 8
-    far_c, far_l = (0, 4) if first else (128, 8)
+    far_c = 0 if first else 128
 
-    d_u = done("du", S.dma_start(T.urep[:, 0:4], T.u[:, 0:4]), 16)
+    d_u = done("du", S.dma_start(T.ub[:, 0:4], T.u[:, 0:4]), 16)
     d_g = done("dgr", Y.dma_start(T.grb[:], T.gr[:]), 16)
 
+    done("v", V.memset(T.zz[:], 0.0))
+    k_wt = done("v", V.memset(T.wt[:], PRED))
     k_eb = done("v", V.memset(T.eb[:], 1.0))
-    k_wt = done("v", V.memset(T.wt[:], 1.0))
-    done("p", g.iota(T.i32[:], [[1, 32]], 0, 0, allow_small_or_imprecise_dtypes=True))
-    done("p", g.iota(T.coln[:], [[128, 2]], 0, 1, allow_small_or_imprecise_dtypes=True))
-    done("p", g.iota(T.ai[:], [[0, 2], [1, 4], [0, 4]], 0, 0, allow_small_or_imprecise_dtypes=True))
+
+    def iota(buf, pattern, base, cm):
+        return done("p", g.iota(buf, pattern, base, cm, allow_small_or_imprecise_dtypes=True))
+
     k_p = done("p", g.iota(T.pi[:, 0:1], [[1, 1]], 0, 1))
+    iota(T.ai[:], [[0, 2], [1, 4], [0, 4]], 0, 0)
+    k_b = iota(T.bi[:], [[0, 2], [1, 16]], 0, 0)
     need("p", k_wt)
-    k_wt = done("p", g.affine_select(T.wt[:], T.wt[:], [[0, 2], [-1, 128]], A.is_gt, PRED, 0, 1))
+    k_wt = done("p", g.affine_select(T.wt[:], T.wt[:], [[-1, 128]], A.is_gt, 1.0, 0, 1))
     need("p", k_eb)
     k_eb = done("p", g.affine_select(T.eb[:, 0:516], T.eb[:, 0:516], [[-1, 516]], A.is_equal, 0.0, 3, 4))
-    done("v", V.memset(T.hb[:], 0.0))
-    done("v", V.memset(T.r4[:], 1.0))
-    k = done("v", V.memset(T.r8[:], 1.0))
-    done("v", V.memset(T.wx[:], 0.0))
-    need("v", k)
-    done("v", V.memset(T.r4[:, 0:32:4], 0.0))
-    done("v", V.memset(T.r8[:, 0:32:8], 0.0))
-    done("v", V.memset(T.r8[:, 4:32:8], 256.0))
+    iota(T.i32[:], [[1, 32]], 0, 0)
+    k_c = iota(T.coln[:], [[128, 2]], 0, 1)
+    k_kk = iota(T.kk[:], [[0, 8], [1, 4]], 0, 0)
+    k_en = iota(T.ent[:], [[1, 256]], 1, 0)
     need("v", k_p)
-    k = done("v", V.tensor_scalar(T.pi[:, 1:2], T.pi[:, 0:1], 3, None, A.bitwise_and))
+    done("v", V.tensor_scalar(T.pi[:, 1:2], T.pi[:, 0:1], 3, None, A.bitwise_and))
+    done("v", V.tensor_scalar(T.pi[:, 2:3], T.pi[:, 0:1], 2, 3, A.logical_shift_right, A.bitwise_and))
+    k = done("v", V.tensor_scalar(T.pi[:, 3:4], T.pi[:, 0:1], 15, None, A.bitwise_and))
+    done("v", V.memset(T.r4[:], 1.0))
+    k1 = done("v", V.memset(T.r16[:], 1.0))
     need("v", k)
-    k = done("v", V.tensor_copy(T.p4[:, 0:1], T.pi[:, 1:2]))
+    k = done("v", V.tensor_copy(T.pf[:, 0:3], T.pi[:, 1:4]))
+    p4 = T.pf[:, 0:1]
+    done("v", V.memset(T.hb[:], 0.0))
     need("v", k)
-    done("v", V.tensor_scalar(T.mk[:], T.ai[:], T.p4[:, 0:1], None, A.is_equal))
+    k_uo = done("v", V.tensor_scalar(T.uo[:], T.zz[:], p4, None, A.add))
+    done("v", V.memset(T.r4[:, 0:32:4], 0.0))
+    done("v", V.memset(T.r16[:, 0:32:16], 0.0))
+    done("v", V.memset(T.wx[:], 0.0))
+    done("v", V.memset(T.lf[:], 0.0))
+    done("v", V.memset(T.lm[:], 0.0))
+    done("v", V.memset(T.tv[:, 0:4], 0.0))
+    need("v", k_b)
+    done("v", V.tensor_scalar(T.mk[:, 0:32], T.ai[:], p4, None, A.is_equal))
+    done("v", V.tensor_scalar(T.mk[:, 32:64], T.bi[:], T.pf[:, 2:3], None, A.is_equal))
 
-    need("v", d_u)
-    w = 4
-    while w < 512:
-        k = done("v", V.tensor_copy(T.urep[:, w:2 * w], T.urep[:, 0:w]))
-        need("v", k)
-        w *= 2
+    need("s", d_u, k_uo)
+    a_u = done("s", S.activation(T.urep[:, 256:512], T.ub[:, 0:4].indirect(T.uo[:, 0:16]), AF.Copy))
+    need("v", d_u, k_uo)
+    k = done("v", V.tensor_copy(T.urep[:, 0:256], T.ub[:, 0:4].indirect(T.uo[:, 0:16])))
+    need("v", k, a_u)
     k_u = done("v", V.quantize_mx(T.uq[:], T.us[:], T.urep[:]))
     need("v", d_g)
     k_g = done("v", V.quantize_mx(T.gq[:], T.gs[:], T.grb[:]))
 
     need("t", k_u, k_g)
-    t_f = done("t", P.matmul_mx(T.pa[:, 0:256], T.uq[:], T.us[:], T.gq[:], T.gs[:], True, True))
-    t_0 = done("t", P.matmul_mx(T.pa[:, 512:640], T.gq[:, 0:128], T.gs[:, 0:128], T.uq[:], T.us[:], True, True))
+    done("t", P.matmul_mx(T.pa[:, 512:640], T.gq[:, 0:128], T.gs[:, 0:128], T.uq[:], T.us[:], True, True))
     t_1 = done("t", P.matmul_mx(T.pa[:, 1024:1152], T.gq[:, 128:256], T.gs[:, 128:256], T.uq[:], T.us[:], True, True))
+    t_f = done("t", P.matmul_mx(T.pa[:, 0:256], T.uq[:], T.us[:], T.gq[:], T.gs[:], True, True))
+    need("s", t_1)
+    a_c = done("s", S.activation(T.sth[:, 0:2], T.pa[:, 512:1025:512], AF.Abs, bias=TINY))
     need("s", t_f)
     a_f = done("s", S.activation(T.ab[:], T.pa[:, 0:256], AF.Abs, bias=TINY))
-    need("v", t_0)
-    done("v", V.tensor_reduce(T.sraw[:, 0:1], T.pa[:, 512:513], X, A.max, apply_absolute_value=True))
-    need("v", t_1)
-    k = done("v", V.tensor_reduce(T.sraw[:, 1:2], T.pa[:, 1024:1025], X, A.max, apply_absolute_value=True))
-    need("v", k)
-    k_th = done("v", V.tensor_scalar(T.sth[:, 0:2], T.sraw[:, 0:2], TINY, None, A.max))
+    a_e = done("s", S.activation(T.erb[:], T.grb[:], AF.Copy)) if not need("s", d_g) else None
+    need("v", k_eb)
+    for b in range(4):
+        k_e = done("v", V.quantize_mx(T.eq[:, 128 * b:128 * b + 128], T.es[:, 128 * b:128 * b + 128], T.eb[:, 3 - b:515 - b]))
 
-    need("v", a_f, k_wt)
-    k_d = done("v", V.tensor_tensor(T.ad[:], T.ab[:], T.wt[:], A.mult))
-    need("v", k_th)
     s0, s1 = T.sth[:, 0:1], T.sth[:, 1:2]
+    need("v", a_c, k_wt)
+    done("v", V.tensor_scalar(T.th[:, 0:128], T.wt[:], s0, None, A.mult))
+    k_d = done("v", V.tensor_scalar(T.th[:, 128:256], T.wt[:], s1, None, A.mult))
+    need("v", a_f)
     done("v", V.tensor_scalar(T.cmp[:, 128:256], T.ab[:, 128:256], s0, None, A.is_gt))
     done("v", V.tensor_scalar(T.cmp[:, 256:384], T.ab[:, 0:128], s1, None, A.is_ge))
     need("v", k_d)
-    k0 = done("v", V.tensor_scalar(T.cmp[:, 0:128], T.ad[:, 0:128], s0, None, A.is_ge))
-    k1 = done("v", V.tensor_scalar(T.cmp[:, 384:512], T.ad[:, 128:256], s1, None, A.is_ge))
+    k0 = done("v", V.tensor_tensor(T.cmp[:, 0:128], T.ab[:, 0:128], T.th[:, 0:128], A.is_gt))
+    k1 = done("v", V.tensor_tensor(T.cmp[:, 384:512], T.ab[:, 128:256], T.th[:, 128:256], A.is_gt))
     need("v", k0)
     k0 = done("v", V.tensor_tensor_scan(T.rks[:, 0:128], T.cmp[:, 0:128], T.cmp[:, 128:256], 0.0, A.add, A.add))
     need("v", k1)
     k1 = done("v", V.tensor_tensor_scan(T.rks[:, 128:256], T.cmp[:, 256:384], T.cmp[:, 384:512], 0.0, A.add, A.add))
     rk = [T.rks[:, 127:128], T.rks[:, 255:256]]
 
-    need("v", k_p, k0)
+    need("v", k_c, k0)
     done("v", V.tensor_scalar(T.vv[:, 0:32], T.i32[:], rk[0], T.coln[:, 0:1], A.is_equal, A.mult))
     need("v", k1)
     k = done("v", V.tensor_scalar(T.vv[:, 32:64], T.i32[:], rk[1], T.coln[:, 1:2], A.is_equal, A.mult))
@@ -161,145 +182,205 @@ def rank_program(g, core, T, topo):
     need("v", k)
     k = done("v", V.transpose(T.xt[:], T.xx[:]))
     need("v", k)
-    k4 = done("v", V.tensor_tensor_scan(T.sg4[:], T.r4[:], T.xt[:], 0.0, A.mult, A.add))
-    k8 = done("v", V.tensor_tensor_scan(T.sg8[:], T.r8[:], T.xt[:], 0.0, A.mult, A.add))
+    k4 = done("v", V.tensor_tensor_scan(T.sg4[:], T.r4[:], T.xt[:, 0:32], 0.0, A.mult, A.add))
+    k8 = done("v", V.tensor_tensor_scan(T.sg16[:], T.r16[:], T.xt[:, 32:64], 0.0, A.mult, A.add))
     need("v", k4)
-    k_o = done("v", V.tensor_scalar(T.ofo[:], T.sg4[:, 3:32:4], 4.0, T.p4[:, 0:1], A.mult, A.add))
+    k_o = done("v", V.tensor_scalar(T.ofo[:], T.sg4[:, 3:32:4], 4.0, p4, A.mult, A.add))
     need("v", k8)
-    k_lp = done("v", V.tensor_copy(T.lp[:, lown:lown + 4], T.sg8[:, 7:32:8]))
+    k_lp = done("v", V.tensor_copy(T.lp[:, 0:2], T.sg16[:, 15:32:16]))
     need("v", k_o)
     h0 = 4 * (own0 - q0)
     k = done("v", V.tensor_copy(T.hb[:, h0:h0 + 128], T.grb[:, 0:1024].indirect(T.ofo[:, 0:8])))
     need("v", k)
     k_q = done("v", V.quantize_mx(T.qb[:, q0:q0 + 128], T.qs[:, q0:q0 + 128], T.hb[:]))
 
-    rid, pid = topo.addr(partner, core)
     b8 = dt.uint8
 
+    def ids(cores):
+        a = [topo.addr(c, core) for c in cores]
+        return [DstId(rid=r_, pnc=p_) for r_, p_ in a]
+
     def hop1(out, in_, sem):
+        rid, pid = topo.addr(partner, core)
         g.remote_dma(out_ap=out, in_ap=in_, remote_sem=T.sem[sem], local_sem=T.sem.sent, pid=pid, routing_id=rid, dma_engine_mask=m1)
         cnt["sent"] += n1
 
-    def hop2(dst, src, sem):
-        ids, outs = [], []
-        for c in peers:
-            r_, p_ = topo.addr(c, core)
-            ids.append(DstId(rid=r_, pnc=p_))
-            outs.append(dst(slot(core, c)))
-        g.remote_dma_fused([RemoteDMATransfer(dst_ids=ids, dma_engine_mask=m2, remote_sem=T.sem[sem], srcs=[src], dsts=outs)], local_sem=T.sem.sent)
-        cnt["sent"] += n2
+    def hop2(dst, src, sem, local):
+        g.remote_dma_fused([RemoteDMATransfer(dst_ids=ids(peers), dma_engine_mask=m2, remote_sem=T.sem[sem], srcs=[src],
+                                              dsts=[dst(slot(me, pair(c))) for c in peers])], local_sem=T.sem[local])
+        cnt[local] += n2
 
-    L1, C1, S1 = ("l1", n1), ("c1", n1), ("s1", n1)
-    L2, C2, S2 = ("l2", 3 * n2), ("c2", 3 * n2), ("s2", 3 * n2)
+    LL, C1, S1 = ("l1", n1 + len(others) * n2), ("c1", n1), ("s1", n1)
+    C2, S2 = ("c2", 3 * n2), ("s2", 3 * n2)
     need("p", k_lp)
-    hop1(T.lp[:, far_l:far_l + 4], T.lp[:, lown:lown + 4], "l1")
+    mine = T.ll[:, 2 * rank:2 * rank + 2]
+    g.remote_dma_fused([
+        RemoteDMATransfer(dst_ids=ids(others), dma_engine_mask=m2, remote_sem=T.sem.l1, srcs=[T.lp[:, 0:2]], dsts=[mine for c in others]),
+        RemoteDMATransfer(dst_ids=ids([partner]), dma_engine_mask=m1, remote_sem=T.sem.l1, srcs=[T.lp[:, 0:2]], dsts=[mine]),
+    ], local_sem=T.sem.sent)
+    cnt["sent"] += n1 + n2
     need("p", k_q)
     hop1(T.qb[:, far_c:far_c + 32].bitcast(b8), T.qb[:, own0:own0 + 32].bitcast(b8), "c1")
     hop1(T.qs[:, far_c:far_c + 32], T.qs[:, own0:own0 + 32], "s1")
-    need("p", L1)
-    hop2(lambda i: T.ll[:, 8 * i:8 * i + 8], T.lp[:, 4:12], "l2")
     need("p", C1)
-    hop2(lambda i: T.cb[:, 64 * i:64 * i + 64].bitcast(b8), T.qb[:, pair0:pair0 + 64].bitcast(b8), "c2")
+    hop2(lambda i: T.cb[:, 64 * i:64 * i + 64].bitcast(b8), T.qb[:, pair0:pair0 + 64].bitcast(b8), "c2", "sent")
     need("p", S1)
-    hop2(lambda i: T.cs[:, 64 * i:64 * i + 64], T.qs[:, pair0:pair0 + 64], "s2")
-
-    need("s", d_g)
-    a_e = done("s", S.activation(T.erb[:], T.grb[:], AF.Copy))
-    need("v", k_eb)
-    for b in range(4):
-        k_e = done("v", V.quantize_mx(T.eq[:, 128 * b:128 * b + 128], T.es[:, 128 * b:128 * b + 128], T.eb[:, 3 - b:515 - b]))
-    done("v", V.tensor_copy(T.rkf[:, 0:1], rk[0]))
-    k = done("v", V.tensor_copy(T.rkf[:, 1:2], rk[1]))
-    k_z = done("v", V.memset(T.acb[:], 0.0))
-    need("v", k)
-    for h in range(2):
-        k = done("v", V.tensor_scalar(T.wv[:, 32 * h:32 * h + 32], T.i32[:], T.rkf[:, h:h + 1], T.sraw[:, h:h + 1], A.is_equal, A.mult))
-    need("v", k)
-    k = done("v", V.transpose(T.wt2[:], T.wv[:]))
-    need("v", k)
-    for a in range(4):
-        k = done("v", V.tensor_reduce(T.wq[0:32, a:a + 1], T.wt2[32 * a:32 * a + 32, :], X, A.add))
-    need("v", k)
-    k = done("v", V.tensor_reduce(T.wx[0:32, 0:1], T.wq[0:32, 0:4], X, A.add))
-    need("v", k)
-    k_sc = done("v", V.transpose(T.wy[0:32, :], T.wx[0:32, :]))
-    need("y", k_sc)
-    d_sc = done("dsc", Y.dma_start(T.sc[:], T.wy[0:1, :]), 16)
+    hop2(lambda i: T.cs[:, 64 * i:64 * i + 64], T.qs[:, pair0:pair0 + 64], "s2", "left")
 
     def decode(ps, n, codes, scales):
         return [done("t", P.matmul_mx(ps[:, 512 * b:512 * b + n], T.eq[:, 128 * b:128 * b + 128], T.es[:, 128 * b:128 * b + 128],
                                       codes, scales, True, True)) for b in range(4)]
 
-    need("t", k_e, a_f, k_th, C1, S1)
-    td = decode(T.pa, 128, T.qb[:, dec0:dec0 + 128], T.qs[:, dec0:dec0 + 128])
-    c0 = pair0 - dec0
-    va = []
-    for b in range(4):
-        src, dst = T.pa[:, 512 * b + c0:512 * b + c0 + 64], T.vb[:, b:256:4]
+    def empty(b, dst, src, td):
         if b % 2:
             need("s", td[b])
-            va.append(done("s", S.activation(dst, src, AF.Copy)))
-        else:
-            need("v", td[b])
-            va.append(done("v", V.tensor_copy(dst, src)))
-    o = 0 if first else 128
-    need("v", a_e, *va)
-    k = done("v", V.tensor_tensor(T.te[:], T.erb[:, 0:1024].indirect(T.ofo[:, 0:8]), T.vb[:, o:o + 128], A.subtract))
+            return done("s", S.activation(dst, src, AF.Copy))
+        need("v", td[b])
+        return done("v", V.tensor_copy(dst, src))
+
+    need("t", k_e, a_f, k_q)
+    td = decode(T.pa, 128, T.qb[:, q0:q0 + 128], T.qs[:, q0:q0 + 128])
+    vo = [empty(b, T.vo[:, b:128:4], T.pa[:, 512 * b + own0 - q0:512 * b + own0 - q0 + 32], td) for b in range(4)]
+    need("v", a_e, *vo)
+    k = done("v", V.tensor_tensor(T.te[:], T.erb[:, 0:1024].indirect(T.ofo[:, 0:8]), T.vo[:], A.subtract))
     need("v", k)
     k_er = done("v", V.tensor_copy(T.erb[:, 0:1024].indirect(T.ofo[:, 0:8]), T.te[:]))
-    need("y", k_er)
+    need("y", k_er, ("left", n2))
     d_er = done("der", Y.dma_start(T.er[:], T.erb[:]), 16)
 
-    need("v", L1, k_lp)
-    k = done("v", V.tensor_copy(T.li[:, 8 * me:8 * me + 8], T.lp[:, 4:12]))
-    need("v", L2)
-    if me > 0:
-        k = done("v", V.tensor_copy(T.li[:, 0:8 * me], T.ll[:, 0:8 * me]))
-    if me < 3:
-        k = done("v", V.tensor_copy(T.li[:, 8 * me + 8:32], T.ll[:, 8 * me:24]))
+    need("t", C1, S1, *vo)
+    td = decode(T.pa, 128, T.qb[:, dec0:dec0 + 128], T.qs[:, dec0:dec0 + 128])
+    c0 = pair0 - dec0
+    for b in range(4):
+        need("s", td[b])
+        a_p = done("s", S.activation(T.vb[:, b:256:4], T.pa[:, 512 * b + c0:512 * b + c0 + 64], AF.Copy))
+
+    d_sc = []
+
+    def fill():
+        done("v", V.tensor_scalar(T.pf[:, 3:4], T.pi[:, 2:3], 1.0, None, A.add))
+        yield
+        c = done("v", V.tensor_scalar(T.pf[:, 4:5], T.pi[:, 2:3], 3.0, 4.0, A.is_equal, A.mult))
+        yield
+        done("v", V.tensor_copy(T.rkf[:, 0:1], rk[0]))
+        w = done("v", V.tensor_copy(T.rkf[:, 1:2], rk[1]))
+        yield
+        need("v", c)
+        done("v", V.tensor_scalar(T.pf[:, 5:6], T.pf[:, 4:5], 4.0 / HOLD, None, A.max))
+        done("v", V.tensor_scalar(T.ce[:], T.kk[:], T.pf[:, 3:4], HOLD, A.is_equal, A.mult))
+        yield
+        c = done("v", V.tensor_scalar(T.cg[:], T.kk[:], T.pf[:, 3:4], None, A.is_gt))
+        yield
+        need("v", w)
+        done("v", V.tensor_scalar(T.wv[:, 0:32], T.i32[:], T.rkf[:, 0:1], T.sth[:, 0:1], A.is_equal, A.mult))
+        w = done("v", V.tensor_scalar(T.wv[:, 32:64], T.i32[:], T.rkf[:, 1:2], T.sth[:, 1:2], A.is_equal, A.mult))
+        yield
+        need("v", c)
+        c = done("v", V.tensor_tensor(T.ch[:, 0:32], T.ce[:], T.cg[:], A.max))
+        yield
+        need("v", w)
+        w = done("v", V.transpose(T.wt2[:], T.wv[:]))
+        yield
+        need("v", c)
+        c = done("v", V.tensor_copy(T.ch[:, 32:64], T.ch[:, 0:32]))
+        yield
+        need("v", w)
+        done("v", V.tensor_reduce(T.wq[0:32, 0:1], T.wt2[0:32, :], X, A.add))
+        done("v", V.tensor_reduce(T.wq[0:32, 1:2], T.wt2[32:64, :], X, A.add))
+        yield
+        need("v", c)
+        c = done("v", V.tensor_copy(T.ch[:, 64:128], T.ch[:, 0:64]))
+        yield
+        done("v", V.tensor_reduce(T.wq[0:32, 2:3], T.wt2[64:96, :], X, A.add))
+        w = done("v", V.tensor_reduce(T.wq[0:32, 3:4], T.wt2[96:128, :], X, A.add))
+        yield
+        need("v", c)
+        done("v", V.tensor_copy(T.ch[:, 128:256], T.ch[:, 0:128]))
+        yield
+        need("v", w)
+        w = done("v", V.tensor_reduce(T.wx[0:32, 0:1], T.wq[0:32, 0:4], X, A.add))
+        yield
+        need("v", w)
+        w = done("v", V.tensor_scalar(T.wx[0:32, 0:1], T.wx[0:32, 0:1], TINY, None, A.subtract))
+        yield
+        need("v", w)
+        w = done("v", V.transpose(T.wy[0:32, :], T.wx[0:32, :]))
+        need("y", w)
+        d_sc.append(done("dsc", Y.dma_start(T.sc[:], T.wy[0:1, :]), 16))
+
+    def lst(s):
+        return T.lp[:, 0:2] if s == rank else T.ll[:, 2 * s:2 * s + 2]
+
+    beside = fill()
+    need("v", k_en, k_lp, LL)
+    for s in range(8):
+        if s:
+            need("v", k)
+            k = done("v", V.tensor_copy(T.pr[:, 32 * s:32 * s + 32], T.lm[:, 0:256].indirect(lst(s))))
+            next(beside, None)
+            need("v", k)
+        k = done("v", V.tensor_copy(T.lm[:, 0:256].indirect(lst(s)), T.ent[:, 32 * s:32 * s + 32]))
+        next(beside, None)
+    k_hp = done("v", V.tensor_tensor_scan(T.hp[:, 0:224], T.ch[:, 0:224], T.pr[:, 32:256], 0.0, A.mult, A.add))
     need("v", k)
-    done("v", V.tensor_scalar(T.l8[:, 0:64:2], T.li[:], 8, None, A.logical_shift_right))
-    k = done("v", V.tensor_scalar(T.l8[:, 1:64:2], T.li[:], 255, None, A.bitwise_and))
-    need("v", k)
-    k_of = done("v", V.tensor_scalar(T.off[:], T.l8[:], 4.0, T.p4[:, 0:1], A.mult, A.add))
-    k = done("v", V.tensor_copy(T.lf[0:32, :], T.l8[0:32, :]))
-    need("v", k)
-    k = done("v", V.transpose(T.nt[0:32, :], T.lf[0:32, :]))
-    need("v", k)
-    done("v", V.tensor_copy(T.nc[0:32, 0:4], T.nt[0:32, 0:16:4]))
-    k_nb = done("v", V.tensor_copy(T.nc[0:32, 4:8], T.nt[0:32, 32:48:4]))
-    need("y", k_nb)
-    done("dnb", Y.dma_start(T.nb[0:4, :], T.nc[0:32, 0:4]), 16)
-    d_nb = done("dnb", Y.dma_start(T.nb[4:8, :], T.nc[0:32, 4:8]), 16)
+    k_hl = done("v", V.tensor_tensor_scan(T.hl[:], T.ch[:], T.lm[:], 0.0, A.mult, A.add))
+    need("v", k_hp)
+    k_op = done("v", V.tensor_scalar(T.offp[:], T.hp[:, 3:224:4], T.pf[:, 5:6], p4, A.mult, A.add))
+    need("v", k_hl)
+    k_ol = done("v", V.tensor_scalar(T.offl[:], T.hl[:, 3:256:4], T.pf[:, 5:6], p4, A.mult, A.add))
+    for x in beside:
+        need("v", k_ol)
 
     need("t", C2, S2)
     td = decode(T.pb, 192, T.cb[:], T.cs[:])
-    vl = []
-    for b in (1, 3):
-        need("s", td[b])
-        vl.append(done("s", S.activation(T.vb[:, 256 + b:1024:4], T.pb[:, 512 * b:512 * b + 192], AF.Copy)))
 
-    need("v", k_of, k_z)
-    emptied = False
+    def landed(banks):
+        return [empty(b, T.vb[:, 256 + b:1024:4], T.pb[:, 512 * b:512 * b + 192], td) for b in banks]
+
+    vl = landed((1, 3))
+
+    def lists(a, b, buf, at):
+        return lambda: done("v", V.tensor_copy(T.lf[0:32, a:b], buf[0:32, at:at + b - a]))
+
+    nbs = [lists(2 * rank, 2 * rank + 2, T.lp, 0)]
+    if rank > 0:
+        nbs.append(lists(0, 2 * rank, T.ll, 0))
+    if rank < 7:
+        nbs.append(lists(2 * rank + 2, 16, T.ll, 2 * rank + 2))
+    nbs += [None, lambda: done("v", V.transpose(T.nt[0:32, :], T.lf[0:32, :]))]
+
+    need("v", k_op)
+    emptied, k_nb = False, None
     for s in range(8):
         m = s // 2
-        if m != me and not emptied:
+        if m == me:
+            need("v", a_p)
+        elif not emptied:
             emptied = True
-            for b in (0, 2):
-                need("v", td[b])
-                vl.append(done("v", V.tensor_copy(T.vb[:, 256 + b:1024:4], T.pb[:, 512 * b:512 * b + 192])))
+            vl += landed((0, 2))
             need("v", *vl)
-        at = (s % 2) if m == me else 2 + 2 * (m - (1 if m > me else 0)) + s % 2
-        v = T.vb[:, 128 * at:128 * at + 128]
-        win = T.acb[:, 0:1024].indirect(T.off[:, 8 * s:8 * s + 8])
+        at = (s % 2) if m == me else 2 + 2 * slot(m, me) + s % 2
+        v, out = T.vb[:, 128 * at:128 * at + 128], T.tv[:, 4 + 128 * s:132 + 128 * s]
         if s:
             need("v", k)
-            k = done("v", V.tensor_tensor(T.tm[:], win, v, A.add))
-            need("v", k)
-            v = T.tm[:]
-        k = done("v", V.tensor_copy(win, v))
-    need("y", k)
-    d_ac = done("dac", Y.dma_start(T.acc[:], T.acb[:]), 16)
+            k = done("v", V.tensor_tensor(out, T.tv[:, 0:4 + 128 * s].indirect(T.offp[:, 8 * s - 8:8 * s]), v, A.add))
+        else:
+            k = done("v", V.tensor_copy(out, v))
+        if nbs:
+            f = nbs.pop(0)
+            if f is not None:
+                k_nb = f()
+    need("v", k_ol, k)
+    need("s", k_ol, k)
+    win, parts = T.tv[:, 0:1028], []
+    for i in range(2):
+        parts.append((256 * i, done("v", V.tensor_copy(T.acb[:, 256 * i:256 * i + 256], win.indirect(T.offl[:, 16 * i:16 * i + 16])))))
+        parts.append((512 + 256 * i, done("s", S.activation(T.acb[:, 512 + 256 * i:768 + 256 * i], win.indirect(T.offl[:, 32 + 16 * i:48 + 16 * i]), AF.Copy))))
+    for c, tok in parts:
+        need("y", tok)
+        d_ac = done("dac", Y.dma_start(T.acc[:, c:c + 256], T.acb[:, c:c + 256]), 16)
+    need("y", k_nb)
+    d_nb = done("dnb", Y.dma_start(T.nb[:], T.nt[0:16, 0:16]), 16)
 
-    need("p", d_u, d_g, d_sc, d_er, d_nb, d_ac, L2, C2, S2)
-    need("p", *[(x, cnt[x]) for x in ("v", "s", "t", "p", "sent")])
+    need("p", d_u, d_g, d_er, d_nb, d_ac, LL, C2, S2, *d_sc)
+    need("p", *[(x, cnt[x]) for x in ("v", "s", "t", "p", "sent", "left")])

@@ -5,6 +5,8 @@ K = 32
 TINY = 2.0 ** -120
 PRED = 1.0 - 2.0 ** -24
 HOLD = 2.0 ** 40
+OUT = -4096.0
+BB = 520
 
 F, B, I, U = "float32", "bfloat16", "int32", "uint16"
 C8, S8 = "float8_e4m3fn_x4", "uint8"
@@ -17,33 +19,73 @@ SCRATCH = {
     "qb": ("sbuf", [128, 160], C8), "qs": ("sbuf", [128, 160], S8),
     "cb": ("sbuf", [128, 192], C8), "cs": ("sbuf", [128, 192], S8),
     "lp": ("sbuf", [128, 16], U), "ll": ("sbuf", [128, 16], U), "ofo": ("sbuf", [128, 8], U),
-    "offp": ("sbuf", [128, 56], U), "offl": ("sbuf", [128, 64], U),
+    "offp": ("sbuf", [128, 32], U), "offl": ("sbuf", [128, 64], U),
     "ab": ("sbuf", [128, 256], F), "th": ("sbuf", [128, 256], F), "wt": ("sbuf", [128, 128], F),
     "sth": ("sbuf", [128, 8], F),
     "cmp": ("sbuf", [128, 512], B), "rks": ("sbuf", [128, 256], B), "rkf": ("sbuf", [128, 8], F),
-    "i32": ("sbuf", [128, 32], F), "coln": ("sbuf", [128, 2], B), "pi": ("sbuf", [128, 8], I), "pf": ("sbuf", [128, 8], F),
-    "ai": ("sbuf", [128, 32], F), "bi": ("sbuf", [128, 32], F), "kk": ("sbuf", [128, 32], F),
+    "i32": ("sbuf", [128, 32], F), "coln": ("sbuf", [128, 2], B), "pi": ("sbuf", [128, 8], I), "pf": ("sbuf", [128, 16], F),
+    "ai": ("sbuf", [128, 32], F), "bi": ("sbuf", [128, 32], F), "k4": ("sbuf", [128, 32], F), "k8": ("sbuf", [128, 32], F),
     "mk": ("sbuf", [128, 64], F), "r4": ("sbuf", [128, 32], F), "r16": ("sbuf", [128, 32], F),
-    "ce": ("sbuf", [128, 32], F), "cg": ("sbuf", [128, 32], F), "ch": ("sbuf", [128, 256], B),
-    "vv": ("sbuf", [128, 64], F), "vt": ("sbuf", [128, 64], F), "q4": ("sbuf", [128, 8], F), "rc": ("sbuf", [128, 8], F),
+    "ce": ("sbuf", [128, 64], F), "cg": ("sbuf", [128, 64], F), "ch4": ("sbuf", [128, 256], B), "ch8": ("sbuf", [128, 256], B),
+    "vv": ("sbuf", [128, 64], F), "vt": ("sbuf", [128, 128], F), "q4": ("sbuf", [128, 8], F),
     "xx": ("sbuf", [128, 64], F), "xt": ("sbuf", [128, 64], F), "sg4": ("sbuf", [128, 32], F), "sg16": ("sbuf", [128, 32], F),
-    "wv": ("sbuf", [128, 64], F), "wt2": ("sbuf", [128, 64], F), "wq": ("sbuf", [128, 8], F), "wx": ("sbuf", [128, 32], F),
-    "wy": ("sbuf", [128, 32], F), "zz": ("sbuf", [128, 16], F),
-    "lf": ("sbuf", [128, 32], F), "nt": ("sbuf", [128, 32], F),
-    "ent": ("sbuf", [128, 256], B), "lm": ("sbuf", [128, 256], B), "pr": ("sbuf", [128, 256], B),
-    "hp": ("sbuf", [128, 256], B), "hl": ("sbuf", [128, 256], B),
-    "tv": ("sbuf", [128, 1032], F),
+    "wv": ("sbuf", [128, 64], F), "wt2": ("sbuf", [128, 128], F), "wq": ("sbuf", [128, 8], F), "wx": ("sbuf", [128, 32], F),
+    "wy": ("sbuf", [128, 32], F), "zz": ("sbuf", [128, 16], F), "zt": ("sbuf", [128, 512], B),
+    "lf": ("sbuf", [128, 32], F), "nt": ("sbuf", [128, 32], F), "nu": ("sbuf", [128, 32], F),
+    "ent": ("sbuf", [128, 256], B), "m8": ("sbuf", [128, 2048], B), "rst": ("sbuf", [128, 2048], B), "mp": ("sbuf", [128, 2064], B),
+    "pr": ("sbuf", [128, 256], B), "hp": ("sbuf", [128, 256], B), "hl": ("sbuf", [128, 256], B),
+    "tv": ("sbuf", [128, 1040], F),
     "acb": ("sbuf", [128, 1024], F), "erb": ("sbuf", [128, 1024], F), "vb": ("sbuf", [128, 1024], F),
     "vo": ("sbuf", [128, 128], F), "te": ("sbuf", [128, 128], F),
     "pa": ("psum", [128, 2048], F), "pb": ("psum", [128, 2048], F),
 }
-SEMAPHORES = ["v", "s", "t", "p", "dgr", "du", "dsc", "dnb", "der", "dac", "l1", "c1", "s1", "c2", "s2", "sent", "left"]
+SEMAPHORES = ["v", "s", "t", "p", "dg1", "dg2", "du", "dl", "dh", "dm", "dsc", "dnb", "der", "dac", "l1", "c1", "s1", "c2", "s2", "sent", "left"]
 
 
 def rank_program(g, core, T, topo):
-    rank = T.rank_of(core)
-    if rank is None:
+    chip = topo.cores_of(core)
+    ranks = [c for c in T.cores if c in chip]
+    if not ranks:
         return
+    others = [c for c in T.cores if c not in chip]
+    peers = [c for c in others if topo.die(c) == topo.die(core)]
+    helpers = [h for h in chip if h not in ranks and all(topo.may_write(h, c) for c in others)]
+    if core not in ranks and core not in helpers:
+        return
+
+    def pair(c):
+        return min(T.rank_of(d) for d in T.cores if d in topo.cores_of(c)) // 2
+
+    me = pair(core)
+
+    def slot(src, dst):
+        return src - (1 if src > dst else 0)
+
+    def ids(cores):
+        a = [topo.addr(c, core) for c in cores]
+        return [DstId(rid=r_, pnc=p_) for r_, p_ in a]
+
+    m2 = topo.mask(core, others[0])
+    for c in others:
+        m2 &= topo.mask(core, c)
+    n2 = bin(m2).count("1")
+
+    def hop2(dst, src, sem, local):
+        g.remote_dma_fused([RemoteDMATransfer(dst_ids=ids(peers), dma_engine_mask=m2, remote_sem=T.sem[sem], srcs=[src],
+                                              dsts=[dst(slot(me, pair(c))) for c in peers])], local_sem=T.sem[local])
+
+    if core in helpers:
+        g.wait_ge(T.sem.s1, sum(bin(topo.mask(c, core) & ~m2).count("1") for c in ranks))
+        hop2(lambda i: T.cs[:, 64 * i:64 * i + 64], T.qs[:, 0:64], "s2", "sent")
+        g.wait_ge(T.sem.sent, n2)
+        return
+
+    rank = T.rank_of(core)
+    partner = [c for c in ranks if c != core][0]
+    first = rank < T.rank_of(partner)
+    m1 = topo.mask(core, partner) & ~m2
+    n1 = bin(m1).count("1")
+
     V, S, P, Y = g.vector, g.scalar, g.tensor, g.sync
     Q = {"v": V, "s": S, "t": P, "p": g, "y": Y}
     A, AF, X = AluOpType, ActivationFunctionType, AxisListType.X
@@ -60,24 +102,6 @@ def rank_program(g, core, T, topo):
                 Q[queue].wait_ge(T.sem[sem], n)
                 seen[(queue, sem)] = n
 
-    partner = [c for c in T.cores if c != core and c in topo.cores_of(core)][0]
-    peers = [c for c in T.cores if c not in topo.cores_of(core) and topo.die(c) == topo.die(core)]
-    others = [c for c in T.cores if c not in topo.cores_of(core)]
-    first = rank < T.rank_of(partner)
-
-    def pair(c):
-        return min(T.rank_of(d) for d in T.cores if d in topo.cores_of(c)) // 2
-
-    me = pair(core)
-
-    def slot(src, dst):
-        return src - (1 if src > dst else 0)
-
-    m2 = topo.mask(core, others[0])
-    for c in others:
-        m2 &= topo.mask(core, c)
-    m1 = topo.mask(core, partner) & ~m2
-    n1, n2 = bin(m1).count("1"), bin(m2).count("1")
     q0 = 0 if first else 32
     own0 = 96 if first else 32
     pair0 = 96 if first else 0
@@ -85,79 +109,92 @@ def rank_program(g, core, T, topo):
     far_c = 0 if first else 128
 
     d_u = done("du", S.dma_start(T.ub[:, 0:4], T.u[:, 0:4]), 16)
-    d_g = done("dgr", Y.dma_start(T.grb[:], T.gr[:]), 16)
-
-    done("v", V.memset(T.zz[:], 0.0))
-    k_wt = done("v", V.memset(T.wt[:], PRED))
-    k_eb = done("v", V.memset(T.eb[:], 1.0))
+    d_1 = done("dg1", Y.dma_start(T.grb[:, 0:512], T.gr[:, 0:512]), 16)
+    d_2 = done("dg2", Y.dma_start(T.grb[:, 512:1024], T.gr[:, 512:1024]), 16)
 
     def iota(buf, pattern, base, cm):
         return done("p", g.iota(buf, pattern, base, cm, allow_small_or_imprecise_dtypes=True))
 
+    done("v", V.memset(T.zz[:], 0.0))
+    k_wt = done("v", V.memset(T.wt[:], PRED))
+    k_eb = done("v", V.memset(T.eb[:], 1.0))
     k_p = done("p", g.iota(T.pi[:, 0:1], [[1, 1]], 0, 1))
-    iota(T.ai[:], [[0, 2], [1, 4], [0, 4]], 0, 0)
-    k_b = iota(T.bi[:], [[0, 2], [1, 16]], 0, 0)
+    k_i = iota(T.i32[:], [[1, 32]], 0, 0)
     need("p", k_wt)
     k_wt = done("p", g.affine_select(T.wt[:], T.wt[:], [[-1, 128]], A.is_gt, 1.0, 0, 1))
     need("p", k_eb)
     k_eb = done("p", g.affine_select(T.eb[:, 0:516], T.eb[:, 0:516], [[-1, 516]], A.is_equal, 0.0, 3, 4))
-    iota(T.i32[:], [[1, 32]], 0, 0)
+    iota(T.ai[:], [[0, 2], [1, 4], [0, 4]], 0, 0)
+    k_b = iota(T.bi[:], [[0, 2], [1, 16]], 0, 0)
     k_c = iota(T.coln[:], [[128, 2]], 0, 1)
-    k_kk = iota(T.kk[:], [[0, 8], [1, 4]], 0, 0)
-    k_en = iota(T.ent[:], [[1, 256]], 1, 0)
+    iota(T.k4[:], [[0, 8], [1, 4]], 0, 0)
+    k_kk = iota(T.k8[:], [[0, 4], [1, 8]], 0, 0)
     need("v", k_p)
     done("v", V.tensor_scalar(T.pi[:, 1:2], T.pi[:, 0:1], 3, None, A.bitwise_and))
     done("v", V.tensor_scalar(T.pi[:, 2:3], T.pi[:, 0:1], 2, 3, A.logical_shift_right, A.bitwise_and))
-    k = done("v", V.tensor_scalar(T.pi[:, 3:4], T.pi[:, 0:1], 15, None, A.bitwise_and))
+    done("v", V.tensor_scalar(T.pi[:, 3:4], T.pi[:, 0:1], 15, None, A.bitwise_and))
+    done("v", V.tensor_scalar(T.pi[:, 4:5], T.pi[:, 0:1], 1, None, A.bitwise_and))
+    done("v", V.tensor_scalar(T.pi[:, 5:6], T.pi[:, 0:1], 1, 7, A.logical_shift_right, A.bitwise_and))
+    k = done("v", V.tensor_scalar(T.pi[:, 6:7], T.pi[:, 0:1], 1, 1, A.logical_shift_right, A.bitwise_and))
     done("v", V.memset(T.r4[:], 1.0))
-    k1 = done("v", V.memset(T.r16[:], 1.0))
     need("v", k)
-    k = done("v", V.tensor_copy(T.pf[:, 0:3], T.pi[:, 1:4]))
-    p4 = T.pf[:, 0:1]
-    done("v", V.memset(T.hb[:], 0.0))
+    k = done("v", V.tensor_copy(T.pf[:, 0:6], T.pi[:, 1:7]))
+    p4, pq4, p16, p1, pq8, ph = [T.pf[:, i:i + 1] for i in range(6)]
+    k2 = done("v", V.memset(T.r16[:], 1.0))
     need("v", k)
     k_uo = done("v", V.tensor_scalar(T.uo[:], T.zz[:], p4, None, A.add))
     done("v", V.memset(T.r4[:, 0:32:4], 0.0))
+    need("v", k2)
     done("v", V.memset(T.r16[:, 0:32:16], 0.0))
-    done("v", V.memset(T.wx[:], 0.0))
-    done("v", V.memset(T.lf[:], 0.0))
-    done("v", V.memset(T.lm[:], 0.0))
-    done("v", V.memset(T.tv[:, 0:4], 0.0))
-    need("v", k_b)
-    done("v", V.tensor_scalar(T.mk[:, 0:32], T.ai[:], p4, None, A.is_equal))
-    done("v", V.tensor_scalar(T.mk[:, 32:64], T.bi[:], T.pf[:, 2:3], None, A.is_equal))
+    k_zt = done("v", V.memset(T.zt[:], 0.0))
+    need("y", k_zt)
+    d_h = done("dh", Y.dma_start(T.hb[:], T.zt[:]), 16)
+    for a in range(4):
+        d_m = done("dm", Y.dma_start(T.m8[:, 512 * a:512 * a + 512], T.zt[:]), 16)
+    need("s", k_i)
+    for s in range(8):
+        a_en = done("s", S.activation(T.ent[:, 32 * s:32 * s + 32], T.i32[:], AF.Copy, bias=float(32 * s + 1)))
 
     need("s", d_u, k_uo)
     a_u = done("s", S.activation(T.urep[:, 256:512], T.ub[:, 0:4].indirect(T.uo[:, 0:16]), AF.Copy))
+    for z in (T.tv[:, 0:2], T.tv[:, 514:BB + 2], T.mp[:, 0:1], T.lf[:], T.wx[:]):
+        done("s", S.activation(z, T.i32[:, 0:z.shape[1]], AF.Copy, scale=0.0))
     need("v", d_u, k_uo)
     k = done("v", V.tensor_copy(T.urep[:, 0:256], T.ub[:, 0:4].indirect(T.uo[:, 0:16])))
     need("v", k, a_u)
     k_u = done("v", V.quantize_mx(T.uq[:], T.us[:], T.urep[:]))
-    need("v", d_g)
-    k_g = done("v", V.quantize_mx(T.gq[:], T.gs[:], T.grb[:]))
 
-    need("t", k_u, k_g)
-    done("t", P.matmul_mx(T.pa[:, 512:640], T.gq[:, 0:128], T.gs[:, 0:128], T.uq[:], T.us[:], True, True))
-    t_1 = done("t", P.matmul_mx(T.pa[:, 1024:1152], T.gq[:, 128:256], T.gs[:, 128:256], T.uq[:], T.us[:], True, True))
-    t_f = done("t", P.matmul_mx(T.pa[:, 0:256], T.uq[:], T.us[:], T.gq[:], T.gs[:], True, True))
-    need("s", t_1)
-    a_c = done("s", S.activation(T.sth[:, 0:2], T.pa[:, 512:1025:512], AF.Abs, bias=TINY))
-    need("s", t_f)
-    a_f = done("s", S.activation(T.ab[:], T.pa[:, 0:256], AF.Abs, bias=TINY))
-    a_e = done("s", S.activation(T.erb[:], T.grb[:], AF.Copy)) if not need("s", d_g) else None
-    need("v", k_eb)
-    for b in range(4):
-        k_e = done("v", V.quantize_mx(T.eq[:, 128 * b:128 * b + 128], T.es[:, 128 * b:128 * b + 128], T.eb[:, 3 - b:515 - b]))
+    def tile_e(b):
+        need("v", k_eb)
+        return done("v", V.quantize_mx(T.eq[:, 128 * b:128 * b + 128], T.es[:, 128 * b:128 * b + 128], T.eb[:, 3 - b:515 - b]))
+
+    a_c, a_f = [], []
+    for h in range(2):
+        j = 128 * h
+        need("v", (d_1, d_2)[h])
+        k_g = done("v", V.quantize_mx(T.gq[:, j:j + 128], T.gs[:, j:j + 128], T.grb[:, 512 * h:512 * h + 512]))
+        need("t", k_u, k_g)
+        t_c = done("t", P.matmul_mx(T.pa[:, 1024 * h:1024 * h + 128], T.gq[:, j:j + 128], T.gs[:, j:j + 128], T.uq[:], T.us[:], True, True))
+        t_f = done("t", P.matmul_mx(T.pa[:, 1024 * h + 512:1024 * h + 640], T.uq[:], T.us[:], T.gq[:, j:j + 128], T.gs[:, j:j + 128], True, True))
+        need("s", t_c)
+        a_c.append(done("s", S.activation(T.sth[:, h:h + 1], T.pa[:, 1024 * h:1024 * h + 1], AF.Abs, bias=TINY)))
+        need("s", t_f)
+        a_f.append(done("s", S.activation(T.ab[:, j:j + 128], T.pa[:, 1024 * h + 512:1024 * h + 640], AF.Abs, bias=TINY)))
+        k_e = tile_e(h)
 
     s0, s1 = T.sth[:, 0:1], T.sth[:, 1:2]
-    need("v", a_c, k_wt)
-    done("v", V.tensor_scalar(T.th[:, 0:128], T.wt[:], s0, None, A.mult))
-    k_d = done("v", V.tensor_scalar(T.th[:, 128:256], T.wt[:], s1, None, A.mult))
-    need("v", a_f)
-    done("v", V.tensor_scalar(T.cmp[:, 128:256], T.ab[:, 128:256], s0, None, A.is_gt))
+    need("s", k_wt, a_c[1])
+    a_t = done("s", S.activation(T.th[:, 128:256], T.wt[:], AF.Copy, scale=s1))
+    need("v", a_c[0], k_wt)
+    k_d = done("v", V.tensor_scalar(T.th[:, 0:128], T.wt[:], s0, None, A.mult))
+    k_e = tile_e(2)
+    need("v", a_f[0], k_d)
+    done("v", V.tensor_tensor(T.cmp[:, 0:128], T.ab[:, 0:128], T.th[:, 0:128], A.is_gt))
+    need("v", a_c[1])
     done("v", V.tensor_scalar(T.cmp[:, 256:384], T.ab[:, 0:128], s1, None, A.is_ge))
-    need("v", k_d)
-    k0 = done("v", V.tensor_tensor(T.cmp[:, 0:128], T.ab[:, 0:128], T.th[:, 0:128], A.is_gt))
+    need("v", a_f[1])
+    k0 = done("v", V.tensor_scalar(T.cmp[:, 128:256], T.ab[:, 128:256], s0, None, A.is_gt))
+    need("v", a_t)
     k1 = done("v", V.tensor_tensor(T.cmp[:, 384:512], T.ab[:, 128:256], T.th[:, 128:256], A.is_gt))
     need("v", k0)
     k0 = done("v", V.tensor_tensor_scan(T.rks[:, 0:128], T.cmp[:, 0:128], T.cmp[:, 128:256], 0.0, A.add, A.add))
@@ -165,222 +202,212 @@ def rank_program(g, core, T, topo):
     k1 = done("v", V.tensor_tensor_scan(T.rks[:, 128:256], T.cmp[:, 256:384], T.cmp[:, 384:512], 0.0, A.add, A.add))
     rk = [T.rks[:, 127:128], T.rks[:, 255:256]]
 
+    def ones(h):
+        return done("s", S.activation(T.rst[:, 1024 * h:1024 * h + 1024], T.grb[:], AF.Copy, scale=0.0, bias=1.0))
+
+    need("s", d_1, d_2)
+    ones(0)
+
     need("v", k_c, k0)
     done("v", V.tensor_scalar(T.vv[:, 0:32], T.i32[:], rk[0], T.coln[:, 0:1], A.is_equal, A.mult))
     need("v", k1)
     k = done("v", V.tensor_scalar(T.vv[:, 32:64], T.i32[:], rk[1], T.coln[:, 1:2], A.is_equal, A.mult))
+    need("v", k_b)
+    done("v", V.tensor_scalar(T.mk[:, 0:32], T.ai[:], p4, OUT, A.not_equal, A.mult))
     need("v", k)
-    k = done("v", V.transpose(T.vt[:], T.vv[:]))
+    for a in range(2):
+        k = done("v", V.transpose(T.vt[0:64, 64 * a:64 * a + 64], T.vv[64 * a:64 * a + 64, :]))
+    done("v", V.tensor_scalar(T.mk[:, 32:64], T.bi[:], p16, OUT, A.not_equal, A.mult))
+    need("v", k)
+    k = done("v", V.tensor_reduce(T.q4[0:64, 0:1], T.vt[0:64, :], X, A.add))
     need("v", k)
     for a in range(4):
-        k = done("v", V.tensor_reduce(T.q4[0:32, a:a + 1], T.vt[32 * a:32 * a + 32, :], X, A.add))
-    need("v", k)
-    k = done("v", V.tensor_reduce(T.rc[0:32, 0:1], T.q4[0:32, 0:4], X, A.add))
-    need("v", k)
-    for a in range(4):
-        k = done("v", V.tensor_scalar(T.xx[32 * a:32 * a + 32, :], T.mk[0:32, :], T.rc[0:32, 0:1], None, A.mult))
+        k = done("v", V.tensor_scalar(T.xx[32 * a:32 * a + 32, :], T.mk[0:32, :], T.q4[0:32, 0:1], T.q4[32:64, 0:1], A.add, A.add))
     need("v", k)
     k = done("v", V.transpose(T.xt[:], T.xx[:]))
     need("v", k)
-    k4 = done("v", V.tensor_tensor_scan(T.sg4[:], T.r4[:], T.xt[:, 0:32], 0.0, A.mult, A.add))
-    k8 = done("v", V.tensor_tensor_scan(T.sg16[:], T.r16[:], T.xt[:, 32:64], 0.0, A.mult, A.add))
+    k4 = done("v", V.tensor_tensor_scan(T.sg4[:], T.r4[:], T.xt[:, 0:32], 0.0, A.mult, A.max))
+    k8 = done("v", V.tensor_tensor_scan(T.sg16[:], T.r16[:], T.xt[:, 32:64], 0.0, A.mult, A.max))
     need("v", k4)
     k_o = done("v", V.tensor_scalar(T.ofo[:], T.sg4[:, 3:32:4], 4.0, p4, A.mult, A.add))
     need("v", k8)
-    k_lp = done("v", V.tensor_copy(T.lp[:, 0:2], T.sg16[:, 15:32:16]))
-    need("v", k_o)
+    k_lp = done("v", V.tensor_scalar(T.lp[:, 0:2], T.sg16[:, 15:32:16], 8.0, float(rank), A.mult, A.add))
     h0 = 4 * (own0 - q0)
-    k = done("v", V.tensor_copy(T.hb[:, h0:h0 + 128], T.grb[:, 0:1024].indirect(T.ofo[:, 0:8])))
-    need("v", k)
+    need("s", k_o, d_h)
+    a_h = done("s", S.activation(T.hb[:, h0 + 64:h0 + 128], T.grb[:, 0:1024].indirect(T.ofo[:, 4:8]), AF.Copy))
+    need("v", k_o, d_h)
+    k = done("v", V.tensor_copy(T.hb[:, h0:h0 + 64], T.grb[:, 0:1024].indirect(T.ofo[:, 0:4])))
+    need("v", k, a_h)
     k_q = done("v", V.quantize_mx(T.qb[:, q0:q0 + 128], T.qs[:, q0:q0 + 128], T.hb[:]))
+    a_e = done("s", S.activation(T.erb[:], T.grb[:], AF.Copy))
+    mine = T.ll[:, 2 * rank:2 * rank + 2]
+    need("y", k_lp)
+    d_l = done("dl", Y.dma_start(mine, T.lp[:, 0:2]), 16)
 
     b8 = dt.uint8
-
-    def ids(cores):
-        a = [topo.addr(c, core) for c in cores]
-        return [DstId(rid=r_, pnc=p_) for r_, p_ in a]
-
-    def hop1(out, in_, sem):
-        rid, pid = topo.addr(partner, core)
-        g.remote_dma(out_ap=out, in_ap=in_, remote_sem=T.sem[sem], local_sem=T.sem.sent, pid=pid, routing_id=rid, dma_engine_mask=m1)
-        cnt["sent"] += n1
-
-    def hop2(dst, src, sem, local):
-        g.remote_dma_fused([RemoteDMATransfer(dst_ids=ids(peers), dma_engine_mask=m2, remote_sem=T.sem[sem], srcs=[src],
-                                              dsts=[dst(slot(me, pair(c))) for c in peers])], local_sem=T.sem[local])
-        cnt[local] += n2
-
     LL, C1, S1 = ("l1", n1 + len(others) * n2), ("c1", n1), ("s1", n1)
     C2, S2 = ("c2", 3 * n2), ("s2", 3 * n2)
     need("p", k_lp)
-    mine = T.ll[:, 2 * rank:2 * rank + 2]
     g.remote_dma_fused([
         RemoteDMATransfer(dst_ids=ids(others), dma_engine_mask=m2, remote_sem=T.sem.l1, srcs=[T.lp[:, 0:2]], dsts=[mine for c in others]),
         RemoteDMATransfer(dst_ids=ids([partner]), dma_engine_mask=m1, remote_sem=T.sem.l1, srcs=[T.lp[:, 0:2]], dsts=[mine]),
     ], local_sem=T.sem.sent)
-    cnt["sent"] += n1 + n2
     need("p", k_q)
-    hop1(T.qb[:, far_c:far_c + 32].bitcast(b8), T.qb[:, own0:own0 + 32].bitcast(b8), "c1")
-    hop1(T.qs[:, far_c:far_c + 32], T.qs[:, own0:own0 + 32], "s1")
+    rid, pid = topo.addr(partner, core)
+    g.remote_dma(out_ap=T.qb[:, far_c:far_c + 32].bitcast(b8), in_ap=T.qb[:, own0:own0 + 32].bitcast(b8), remote_sem=T.sem.c1,
+                 local_sem=T.sem.sent, pid=pid, routing_id=rid, dma_engine_mask=m1)
+    hs = 0 if first else 32
+    g.remote_dma_fused([RemoteDMATransfer(dst_ids=ids(helpers + [partner]), dma_engine_mask=m1, remote_sem=T.sem.s1,
+                                          srcs=[T.qs[:, own0:own0 + 32]],
+                                          dsts=[T.qs[:, hs:hs + 32] for h in helpers] + [T.qs[:, far_c:far_c + 32]])], local_sem=T.sem.sent)
+    cnt["sent"] += 3 * n1 + n2
     need("p", C1)
-    hop2(lambda i: T.cb[:, 64 * i:64 * i + 64].bitcast(b8), T.qb[:, pair0:pair0 + 64].bitcast(b8), "c2", "sent")
-    need("p", S1)
-    hop2(lambda i: T.cs[:, 64 * i:64 * i + 64], T.qs[:, pair0:pair0 + 64], "s2", "left")
+    hop2(lambda i: T.cb[:, 64 * i:64 * i + 64].bitcast(b8), T.qb[:, pair0:pair0 + 64].bitcast(b8), "c2", "left")
+    cnt["left"] += n2
+
+    k_e = tile_e(3)
+    f4, f8, e4, e8, x4, x8, pl, ps = [T.pf[:, 6 + i:7 + i] for i in range(8)]
+    need("v", k_kk)
+    done("v", V.tensor_scalar(f4, pq4, 1.0, None, A.add))
+    k = done("v", V.tensor_scalar(f8, pq8, 1.0, None, A.add))
+    done("v", V.tensor_scalar(e4, pq4, 3.0, 2.0, A.is_equal, A.mult))
+    c = done("v", V.tensor_scalar(e8, pq8, 7.0, 2.0, A.is_equal, A.mult))
+    done("v", V.tensor_scalar(pl, ph, float(BB), p1, A.mult, A.add))
+    done("v", V.tensor_scalar(ps, pq8, -0.125, None, A.mult))
+    need("v", k)
+    done("v", V.tensor_scalar(T.ce[:, 0:32], T.k8[:], f8, HOLD, A.is_equal, A.mult))
+    done("v", V.tensor_scalar(T.ce[:, 32:64], T.k4[:], f4, HOLD, A.is_equal, A.mult))
+    done("v", V.tensor_scalar(T.cg[:, 0:32], T.k8[:], f8, None, A.is_gt))
+    k = done("v", V.tensor_scalar(T.cg[:, 32:64], T.k4[:], f4, None, A.is_gt))
+    need("v", c)
+    done("v", V.tensor_scalar(x4, e4, 2.0 / HOLD, None, A.max))
+    done("v", V.tensor_scalar(x8, e8, 2.0 / HOLD, None, A.max))
+    need("v", k)
+    done("v", V.tensor_tensor(T.ch8[:, 0:32], T.ce[:, 0:32], T.cg[:, 0:32], A.max))
+    a_ch = done("v", V.tensor_tensor(T.ch4[:, 0:32], T.ce[:, 32:64], T.cg[:, 32:64], A.max))
 
     def decode(ps, n, codes, scales):
         return [done("t", P.matmul_mx(ps[:, 512 * b:512 * b + n], T.eq[:, 128 * b:128 * b + 128], T.es[:, 128 * b:128 * b + 128],
                                       codes, scales, True, True)) for b in range(4)]
 
-    def empty(b, dst, src, td):
-        if b % 2:
-            need("s", td[b])
+    def empty(q, tok, dst, src):
+        need(q, tok)
+        if q == "s":
             return done("s", S.activation(dst, src, AF.Copy))
-        need("v", td[b])
         return done("v", V.tensor_copy(dst, src))
 
-    need("t", k_e, a_f, k_q)
+    need("t", k_e, a_f[1], k_q)
     td = decode(T.pa, 128, T.qb[:, q0:q0 + 128], T.qs[:, q0:q0 + 128])
-    vo = [empty(b, T.vo[:, b:128:4], T.pa[:, 512 * b + own0 - q0:512 * b + own0 - q0 + 32], td) for b in range(4)]
+    vo = [empty("s" if b % 2 else "v", td[b], T.vo[:, b:128:4], T.pa[:, 512 * b + own0 - q0:512 * b + own0 - q0 + 32]) for b in range(4)]
+    need("s", k1)
+    for h in range(2):
+        a_rk = done("s", S.activation(T.rkf[:, h:h + 1], rk[h], AF.Copy))
+    a_r = ones(1)
     need("v", a_e, *vo)
     k = done("v", V.tensor_tensor(T.te[:], T.erb[:, 0:1024].indirect(T.ofo[:, 0:8]), T.vo[:], A.subtract))
+    need("v", a_rk)
+    done("v", V.tensor_scalar(T.wv[:, 0:32], T.i32[:], T.rkf[:, 0:1], T.sth[:, 0:1], A.is_equal, A.mult))
+    w = done("v", V.tensor_scalar(T.wv[:, 32:64], T.i32[:], T.rkf[:, 1:2], T.sth[:, 1:2], A.is_equal, A.mult))
     need("v", k)
     k_er = done("v", V.tensor_copy(T.erb[:, 0:1024].indirect(T.ofo[:, 0:8]), T.te[:]))
     need("y", k_er, ("left", n2))
     d_er = done("der", Y.dma_start(T.er[:], T.erb[:]), 16)
+    need("v", w)
+    for a in range(2):
+        w = done("v", V.transpose(T.wt2[0:64, 64 * a:64 * a + 64], T.wv[64 * a:64 * a + 64, :]))
+    need("v", a_r)
+    k_r = done("v", V.memset(T.rst[:, 0:2048:8], 0.0))
+    need("v", w)
+    w = done("v", V.tensor_reduce(T.wq[0:64, 0:1], T.wt2[0:64, :], X, A.add))
+    need("v", w)
+    w = done("v", V.tensor_scalar(T.wx[0:32, 0:1], T.wq[0:32, 0:1], T.wq[32:64, 0:1], TINY, A.add, A.subtract))
+    need("v", w)
+    w = done("v", V.transpose(T.wy[0:32, :], T.wx[0:32, :]))
+    need("y", w)
+    d_sc = done("dsc", Y.dma_start(T.sc[:], T.wy[0:1, :]), 16)
+    for n in (32, 64, 128):
+        need("s", a_ch)
+        done("s", S.activation(T.ch8[:, n:2 * n], T.ch8[:, 0:n], AF.Copy))
+        a_ch = done("s", S.activation(T.ch4[:, n:2 * n], T.ch4[:, 0:n], AF.Copy))
 
     need("t", C1, S1, *vo)
     td = decode(T.pa, 128, T.qb[:, dec0:dec0 + 128], T.qs[:, dec0:dec0 + 128])
-    c0 = pair0 - dec0
     for b in range(4):
-        need("s", td[b])
-        a_p = done("s", S.activation(T.vb[:, b:256:4], T.pa[:, 512 * b + c0:512 * b + c0 + 64], AF.Copy))
+        h, i, c0 = b // 2, b % 2, 512 * b + pair0 - dec0
+        if me == 0:
+            empty("s", td[b], T.tv[:, BB * h + 2 + i:BB * h + 66:2], T.pa[:, c0:c0 + 32])
+            a_p = empty("s", td[b], T.vb[:, 512 * h + 64 + i:512 * h + 128:2], T.pa[:, c0 + 32:c0 + 64])
+        else:
+            a_p = empty("s", td[b], T.vb[:, 512 * h + i:512 * h + 128:2], T.pa[:, c0:c0 + 64])
 
-    d_sc = []
-
-    def fill():
-        done("v", V.tensor_scalar(T.pf[:, 3:4], T.pi[:, 2:3], 1.0, None, A.add))
-        yield
-        c = done("v", V.tensor_scalar(T.pf[:, 4:5], T.pi[:, 2:3], 3.0, 4.0, A.is_equal, A.mult))
-        yield
-        done("v", V.tensor_copy(T.rkf[:, 0:1], rk[0]))
-        w = done("v", V.tensor_copy(T.rkf[:, 1:2], rk[1]))
-        yield
-        need("v", c)
-        done("v", V.tensor_scalar(T.pf[:, 5:6], T.pf[:, 4:5], 4.0 / HOLD, None, A.max))
-        done("v", V.tensor_scalar(T.ce[:], T.kk[:], T.pf[:, 3:4], HOLD, A.is_equal, A.mult))
-        yield
-        c = done("v", V.tensor_scalar(T.cg[:], T.kk[:], T.pf[:, 3:4], None, A.is_gt))
-        yield
-        need("v", w)
-        done("v", V.tensor_scalar(T.wv[:, 0:32], T.i32[:], T.rkf[:, 0:1], T.sth[:, 0:1], A.is_equal, A.mult))
-        w = done("v", V.tensor_scalar(T.wv[:, 32:64], T.i32[:], T.rkf[:, 1:2], T.sth[:, 1:2], A.is_equal, A.mult))
-        yield
-        need("v", c)
-        c = done("v", V.tensor_tensor(T.ch[:, 0:32], T.ce[:], T.cg[:], A.max))
-        yield
-        need("v", w)
-        w = done("v", V.transpose(T.wt2[:], T.wv[:]))
-        yield
-        need("v", c)
-        c = done("v", V.tensor_copy(T.ch[:, 32:64], T.ch[:, 0:32]))
-        yield
-        need("v", w)
-        done("v", V.tensor_reduce(T.wq[0:32, 0:1], T.wt2[0:32, :], X, A.add))
-        done("v", V.tensor_reduce(T.wq[0:32, 1:2], T.wt2[32:64, :], X, A.add))
-        yield
-        need("v", c)
-        c = done("v", V.tensor_copy(T.ch[:, 64:128], T.ch[:, 0:64]))
-        yield
-        done("v", V.tensor_reduce(T.wq[0:32, 2:3], T.wt2[64:96, :], X, A.add))
-        w = done("v", V.tensor_reduce(T.wq[0:32, 3:4], T.wt2[96:128, :], X, A.add))
-        yield
-        need("v", c)
-        done("v", V.tensor_copy(T.ch[:, 128:256], T.ch[:, 0:128]))
-        yield
-        need("v", w)
-        w = done("v", V.tensor_reduce(T.wx[0:32, 0:1], T.wq[0:32, 0:4], X, A.add))
-        yield
-        need("v", w)
-        w = done("v", V.tensor_scalar(T.wx[0:32, 0:1], T.wx[0:32, 0:1], TINY, None, A.subtract))
-        yield
-        need("v", w)
-        w = done("v", V.transpose(T.wy[0:32, :], T.wx[0:32, :]))
-        need("y", w)
-        d_sc.append(done("dsc", Y.dma_start(T.sc[:], T.wy[0:1, :]), 16))
-
-    def lst(s):
-        return T.lp[:, 0:2] if s == rank else T.ll[:, 2 * s:2 * s + 2]
-
-    beside = fill()
-    need("v", k_en, k_lp, LL)
-    for s in range(8):
-        if s:
-            need("v", k)
-            k = done("v", V.tensor_copy(T.pr[:, 32 * s:32 * s + 32], T.lm[:, 0:256].indirect(lst(s))))
-            next(beside, None)
-            need("v", k)
-        k = done("v", V.tensor_copy(T.lm[:, 0:256].indirect(lst(s)), T.ent[:, 32 * s:32 * s + 32]))
-        next(beside, None)
-    k_hp = done("v", V.tensor_tensor_scan(T.hp[:, 0:224], T.ch[:, 0:224], T.pr[:, 32:256], 0.0, A.mult, A.add))
+    need("v", LL, d_l, a_en, d_m, a_ch, k_r)
+    k = done("v", V.tensor_copy(T.m8[:, 0:2048].indirect(T.ll[:, 0:16]), T.ent[:]))
+    n = done("v", V.tensor_copy(T.lf[0:32, 0:16], T.ll[0:32, 0:16]))
     need("v", k)
-    k_hl = done("v", V.tensor_tensor_scan(T.hl[:], T.ch[:], T.lm[:], 0.0, A.mult, A.add))
-    need("v", k_hp)
-    k_op = done("v", V.tensor_scalar(T.offp[:], T.hp[:, 3:224:4], T.pf[:, 5:6], p4, A.mult, A.add))
-    need("v", k_hl)
-    k_ol = done("v", V.tensor_scalar(T.offl[:], T.hl[:, 3:256:4], T.pf[:, 5:6], p4, A.mult, A.add))
-    for x in beside:
-        need("v", k_ol)
+    k = done("v", V.tensor_tensor_scan(T.mp[:, 1:2049], T.rst[:], T.m8[:], 0.0, A.mult, A.max))
+    need("v", n)
+    n = done("v", V.transpose(T.nt[0:32, :], T.lf[0:32, :]))
+    need("v", k)
+    k = done("v", V.tensor_copy(T.pr[:, 0:224], T.mp[:, 0:2048].indirect(T.ll[:, 2:16])))
+    need("v", n)
+    k_nb = done("v", V.tensor_scalar(T.nu[0:32, :], T.nt[0:32, :], 0.125, T.pf[0:32, 13:14], A.mult, A.add))
+    need("v", k)
+    k = done("v", V.tensor_tensor_scan(T.hp[:, 0:224], T.ch8[:, 0:224], T.pr[:, 0:224], 0.0, A.mult, A.add))
+    need("v", k)
+    k_op = done("v", V.tensor_scalar(T.offp[:, 0:28], T.hp[:, 7:224:8], x8, p1, A.mult, A.add))
+    need("y", k_nb)
+    d_nb = done("dnb", Y.dma_start(T.nb[:], T.nu[0:16, 0:16]), 16)
 
     need("t", C2, S2)
     td = decode(T.pb, 192, T.cb[:], T.cs[:])
+    got = [[], []]
 
-    def landed(banks):
-        return [empty(b, T.vb[:, 256 + b:1024:4], T.pb[:, 512 * b:512 * b + 192], td) for b in banks]
+    def landed(b, part):
+        h, i, q, n = b // 2, b % 2, "s" if b % 2 else "v", 0 if me == 0 else 32
+        if part == 0 and n:
+            got[h].append(empty(q, td[b], T.tv[:, BB * h + 2 + i:BB * h + 66:2], T.pb[:, 512 * b:512 * b + 32]))
+        if part == 1:
+            got[h].append(empty(q, td[b], T.vb[:, 512 * h + 128 + 2 * n + i:512 * h + 512:2], T.pb[:, 512 * b + n:512 * b + 192]))
 
-    vl = landed((1, 3))
+    for b in (0, 1, 3):
+        landed(b, 0)
+        landed(b, 1)
 
-    def lists(a, b, buf, at):
-        return lambda: done("v", V.tensor_copy(T.lf[0:32, a:b], buf[0:32, at:at + b - a]))
+    last = [None, None]
 
-    nbs = [lists(2 * rank, 2 * rank + 2, T.lp, 0)]
-    if rank > 0:
-        nbs.append(lists(0, 2 * rank, T.ll, 0))
-    if rank < 7:
-        nbs.append(lists(2 * rank + 2, 16, T.ll, 2 * rank + 2))
-    nbs += [None, lambda: done("v", V.transpose(T.nt[0:32, :], T.lf[0:32, :]))]
-
-    need("v", k_op)
-    emptied, k_nb = False, None
-    for s in range(8):
+    def add(h, s):
         m = s // 2
-        if m == me:
-            need("v", a_p)
-        elif not emptied:
-            emptied = True
-            vl += landed((0, 2))
-            need("v", *vl)
         at = (s % 2) if m == me else 2 + 2 * slot(m, me) + s % 2
-        v, out = T.vb[:, 128 * at:128 * at + 128], T.tv[:, 4 + 128 * s:132 + 128 * s]
-        if s:
-            need("v", k)
-            k = done("v", V.tensor_tensor(out, T.tv[:, 0:4 + 128 * s].indirect(T.offp[:, 8 * s - 8:8 * s]), v, A.add))
+        need("v", k_op, a_p, *got[h])
+        if last[h]:
+            need("v", last[h])
+        last[h] = done("v", V.tensor_tensor(T.tv[:, BB * h + 2 + 64 * s:BB * h + 66 + 64 * s],
+                                            T.tv[:, BB * h:BB * h + 2 + 64 * s].indirect(T.offp[:, 4 * s - 4:4 * s]),
+                                            T.vb[:, 512 * h + 64 * at:512 * h + 64 * at + 64], A.add))
+
+    for s in range(1, 10):
+        if s < 8:
+            add(0, s)
+        if s < 3:
+            landed(2, s - 1)
         else:
-            k = done("v", V.tensor_copy(out, v))
-        if nbs:
-            f = nbs.pop(0)
-            if f is not None:
-                k_nb = f()
-    need("v", k_ol, k)
-    need("s", k_ol, k)
-    win, parts = T.tv[:, 0:1028], []
+            add(1, s - 2)
+        if s == 7:
+            k_hl = done("v", V.tensor_tensor_scan(T.hl[:], T.ch4[:], T.mp[:, 8:2049:8], 0.0, A.mult, A.add))
+        if s == 8:
+            need("v", k_hl)
+            k_ol = done("v", V.tensor_scalar(T.offl[:], T.hl[:, 3:256:4], x4, pl, A.mult, A.add))
+
+    need("v", k_ol, *last)
+    need("s", k_ol, *last)
+    win, parts = T.tv[:, 0:BB + 514], []
     for i in range(2):
         parts.append((256 * i, done("v", V.tensor_copy(T.acb[:, 256 * i:256 * i + 256], win.indirect(T.offl[:, 16 * i:16 * i + 16])))))
         parts.append((512 + 256 * i, done("s", S.activation(T.acb[:, 512 + 256 * i:768 + 256 * i], win.indirect(T.offl[:, 32 + 16 * i:48 + 16 * i]), AF.Copy))))
     for c, tok in parts:
-        need("y", tok)
-        d_ac = done("dac", Y.dma_start(T.acc[:, c:c + 256], T.acb[:, c:c + 256]), 16)
-    need("y", k_nb)
-    d_nb = done("dnb", Y.dma_start(T.nb[:], T.nt[0:16, 0:16]), 16)
+        q = "s" if tok == parts[-1][1] else "y"
+        need(q, tok)
+        d_ac = done("dac", Q[q].dma_start(T.acc[:, c:c + 256], T.acb[:, c:c + 256]), 16)
 
-    need("p", d_u, d_g, d_er, d_nb, d_ac, LL, C2, S2, *d_sc)
+    need("p", d_u, d_1, d_2, d_h, d_m, d_l, d_er, d_nb, d_ac, d_sc, LL, C2, S2)
     need("p", *[(x, cnt[x]) for x in ("v", "s", "t", "p", "sent", "left")])

from concourse.bass import DstId, RemoteDMATransfer
from concourse.mybir import dt, AluOpType, AxisListType, ActivationFunctionType

K = 32
TINY = 2.0 ** -120
PRED = 1.0 - 2.0 ** -24
HOLD = 2.0 ** 40
OUT = -4096.0
BB = 520

F, B, I, U = "float32", "bfloat16", "int32", "uint16"
C8, S8 = "float8_e4m3fn_x4", "uint8"
SCRATCH = {
    "grb": ("sbuf", [128, 1024], B), "ub": ("sbuf", [128, 16], B), "urep": ("sbuf", [128, 512], B), "hb": ("sbuf", [128, 512], B),
    "eb": ("sbuf", [128, 528], B), "uo": ("sbuf", [128, 16], U),
    "gq": ("sbuf", [128, 256], C8), "gs": ("sbuf", [128, 256], S8),
    "uq": ("sbuf", [128, 128], C8), "us": ("sbuf", [128, 128], S8),
    "eq": ("sbuf", [128, 512], C8), "es": ("sbuf", [128, 512], S8),
    "qb": ("sbuf", [128, 160], C8), "qs": ("sbuf", [128, 160], S8),
    "cb": ("sbuf", [128, 192], C8), "cs": ("sbuf", [128, 192], S8),
    "lp": ("sbuf", [128, 16], U), "ll": ("sbuf", [128, 16], U), "ofo": ("sbuf", [128, 8], U),
    "offp": ("sbuf", [128, 32], U), "offl": ("sbuf", [128, 64], U),
    "ab": ("sbuf", [128, 256], F), "th": ("sbuf", [128, 256], F), "wt": ("sbuf", [128, 128], F),
    "sth": ("sbuf", [128, 8], F),
    "cmp": ("sbuf", [128, 512], B), "rks": ("sbuf", [128, 256], B), "rkf": ("sbuf", [128, 8], F),
    "i32": ("sbuf", [128, 32], F), "coln": ("sbuf", [128, 2], B), "pi": ("sbuf", [128, 8], I), "pf": ("sbuf", [128, 16], F),
    "ai": ("sbuf", [128, 32], F), "bi": ("sbuf", [128, 32], F), "k4": ("sbuf", [128, 32], F), "k8": ("sbuf", [128, 32], F),
    "mk": ("sbuf", [128, 64], F), "r4": ("sbuf", [128, 32], F), "r16": ("sbuf", [128, 32], F),
    "ce": ("sbuf", [128, 64], F), "cg": ("sbuf", [128, 64], F), "ch4": ("sbuf", [128, 256], B), "ch8": ("sbuf", [128, 256], B),
    "vv": ("sbuf", [128, 64], F), "vt": ("sbuf", [128, 128], F), "q4": ("sbuf", [128, 8], F),
    "xx": ("sbuf", [128, 64], F), "xt": ("sbuf", [128, 64], F), "sg4": ("sbuf", [128, 32], F), "sg16": ("sbuf", [128, 32], F),
    "wv": ("sbuf", [128, 64], F), "wt2": ("sbuf", [128, 128], F), "wq": ("sbuf", [128, 8], F), "wx": ("sbuf", [128, 32], F),
    "wy": ("sbuf", [128, 32], F), "zz": ("sbuf", [128, 16], F), "zt": ("sbuf", [128, 512], B),
    "lf": ("sbuf", [128, 32], F), "nt": ("sbuf", [128, 32], F), "nu": ("sbuf", [128, 32], F),
    "ent": ("sbuf", [128, 256], B), "m8": ("sbuf", [128, 2048], B), "rst": ("sbuf", [128, 2048], B), "mp": ("sbuf", [128, 2064], B),
    "pr": ("sbuf", [128, 256], B), "hp": ("sbuf", [128, 256], B), "hl": ("sbuf", [128, 256], B),
    "tv": ("sbuf", [128, 1040], F),
    "acb": ("sbuf", [128, 1024], F), "erb": ("sbuf", [128, 1024], F), "vb": ("sbuf", [128, 1024], F),
    "vo": ("sbuf", [128, 128], F), "te": ("sbuf", [128, 128], F),
    "pa": ("psum", [128, 2048], F), "pb": ("psum", [128, 2048], F),
}
SEMAPHORES = ["v", "s", "t", "p", "dg1", "dg2", "du", "dl", "dh", "dm", "dsc", "dnb", "der", "dac", "l1", "c1", "s1", "c2", "s2", "sent", "left"]


def rank_program(g, core, T, topo):
    chip = topo.cores_of(core)
    ranks = [c for c in T.cores if c in chip]
    if not ranks:
        return
    others = [c for c in T.cores if c not in chip]
    peers = [c for c in others if topo.die(c) == topo.die(core)]
    helpers = [h for h in chip if h not in ranks and all(topo.may_write(h, c) for c in others)]
    if core not in ranks and core not in helpers:
        return

    def pair(c):
        return min(T.rank_of(d) for d in T.cores if d in topo.cores_of(c)) // 2

    me = pair(core)

    def slot(src, dst):
        return src - (1 if src > dst else 0)

    def ids(cores):
        a = [topo.addr(c, core) for c in cores]
        return [DstId(rid=r_, pnc=p_) for r_, p_ in a]

    m2 = topo.mask(core, others[0])
    for c in others:
        m2 &= topo.mask(core, c)
    n2 = bin(m2).count("1")

    def hop2(dst, src, sem, local):
        g.remote_dma_fused([RemoteDMATransfer(dst_ids=ids(peers), dma_engine_mask=m2, remote_sem=T.sem[sem], srcs=[src],
                                              dsts=[dst(slot(me, pair(c))) for c in peers])], local_sem=T.sem[local])

    if core in helpers:
        g.wait_ge(T.sem.s1, sum(bin(topo.mask(c, core) & ~m2).count("1") for c in ranks))
        hop2(lambda i: T.cs[:, 64 * i:64 * i + 64], T.qs[:, 0:64], "s2", "sent")
        g.wait_ge(T.sem.sent, n2)
        return

    rank = T.rank_of(core)
    partner = [c for c in ranks if c != core][0]
    first = rank < T.rank_of(partner)
    m1 = topo.mask(core, partner) & ~m2
    n1 = bin(m1).count("1")

    V, S, P, Y = g.vector, g.scalar, g.tensor, g.sync
    Q = {"v": V, "s": S, "t": P, "p": g, "y": Y}
    A, AF, X = AluOpType, ActivationFunctionType, AxisListType.X
    cnt, seen = {"sent": 0, "left": 0}, {}

    def done(sem, ins, n=1):
        ins.then_inc(T.sem[sem], n)
        cnt[sem] = cnt.get(sem, 0) + n
        return (sem, cnt[sem])

    def need(queue, *toks):
        for sem, n in toks:
            if seen.get((queue, sem), 0) < n:
                Q[queue].wait_ge(T.sem[sem], n)
                seen[(queue, sem)] = n

    q0 = 0 if first else 32
    own0 = 96 if first else 32
    pair0 = 96 if first else 0
    dec0 = 32 if first else 0
    far_c = 0 if first else 128

    d_u = done("du", S.dma_start(T.ub[:, 0:4], T.u[:, 0:4]), 16)
    d_1 = done("dg1", Y.dma_start(T.grb[:, 0:512], T.gr[:, 0:512]), 16)
    d_2 = done("dg2", Y.dma_start(T.grb[:, 512:1024], T.gr[:, 512:1024]), 16)

    def iota(buf, pattern, base, cm):
        return done("p", g.iota(buf, pattern, base, cm, allow_small_or_imprecise_dtypes=True))

    done("v", V.memset(T.zz[:], 0.0))
    k_wt = done("v", V.memset(T.wt[:], PRED))
    k_eb = done("v", V.memset(T.eb[:], 1.0))
    k_p = done("p", g.iota(T.pi[:, 0:1], [[1, 1]], 0, 1))
    k_i = iota(T.i32[:], [[1, 32]], 0, 0)
    need("p", k_wt)
    k_wt = done("p", g.affine_select(T.wt[:], T.wt[:], [[-1, 128]], A.is_gt, 1.0, 0, 1))
    need("p", k_eb)
    k_eb = done("p", g.affine_select(T.eb[:, 0:516], T.eb[:, 0:516], [[-1, 516]], A.is_equal, 0.0, 3, 4))
    iota(T.ai[:], [[0, 2], [1, 4], [0, 4]], 0, 0)
    k_b = iota(T.bi[:], [[0, 2], [1, 16]], 0, 0)
    k_c = iota(T.coln[:], [[128, 2]], 0, 1)
    iota(T.k4[:], [[0, 8], [1, 4]], 0, 0)
    k_kk = iota(T.k8[:], [[0, 4], [1, 8]], 0, 0)
    need("v", k_p)
    done("v", V.tensor_scalar(T.pi[:, 1:2], T.pi[:, 0:1], 3, None, A.bitwise_and))
    done("v", V.tensor_scalar(T.pi[:, 2:3], T.pi[:, 0:1], 2, 3, A.logical_shift_right, A.bitwise_and))
    done("v", V.tensor_scalar(T.pi[:, 3:4], T.pi[:, 0:1], 15, None, A.bitwise_and))
    done("v", V.tensor_scalar(T.pi[:, 4:5], T.pi[:, 0:1], 1, None, A.bitwise_and))
    done("v", V.tensor_scalar(T.pi[:, 5:6], T.pi[:, 0:1], 1, 7, A.logical_shift_right, A.bitwise_and))
    k = done("v", V.tensor_scalar(T.pi[:, 6:7], T.pi[:, 0:1], 1, 1, A.logical_shift_right, A.bitwise_and))
    done("v", V.memset(T.r4[:], 1.0))
    need("v", k)
    k = done("v", V.tensor_copy(T.pf[:, 0:6], T.pi[:, 1:7]))
    p4, pq4, p16, p1, pq8, ph = [T.pf[:, i:i + 1] for i in range(6)]
    k2 = done("v", V.memset(T.r16[:], 1.0))
    need("v", k)
    k_uo = done("v", V.tensor_scalar(T.uo[:], T.zz[:], p4, None, A.add))
    done("v", V.memset(T.r4[:, 0:32:4], 0.0))
    need("v", k2)
    done("v", V.memset(T.r16[:, 0:32:16], 0.0))
    k_zt = done("v", V.memset(T.zt[:], 0.0))
    need("y", k_zt)
    d_h = done("dh", Y.dma_start(T.hb[:], T.zt[:]), 16)
    for a in range(4):
        d_m = done("dm", Y.dma_start(T.m8[:, 512 * a:512 * a + 512], T.zt[:]), 16)
    need("s", k_i)
    for s in range(8):
        a_en = done("s", S.activation(T.ent[:, 32 * s:32 * s + 32], T.i32[:], AF.Copy, bias=float(32 * s + 1)))

    need("s", d_u, k_uo)
    a_u = done("s", S.activation(T.urep[:, 256:512], T.ub[:, 0:4].indirect(T.uo[:, 0:16]), AF.Copy))
    for z in (T.tv[:, 0:2], T.tv[:, 514:BB + 2], T.mp[:, 0:1], T.lf[:], T.wx[:]):
        done("s", S.activation(z, T.i32[:, 0:z.shape[1]], AF.Copy, scale=0.0))
    need("v", d_u, k_uo)
    k = done("v", V.tensor_copy(T.urep[:, 0:256], T.ub[:, 0:4].indirect(T.uo[:, 0:16])))
    need("v", k, a_u)
    k_u = done("v", V.quantize_mx(T.uq[:], T.us[:], T.urep[:]))

    def tile_e(b):
        need("v", k_eb)
        return done("v", V.quantize_mx(T.eq[:, 128 * b:128 * b + 128], T.es[:, 128 * b:128 * b + 128], T.eb[:, 3 - b:515 - b]))

    a_c, a_f = [], []
    for h in range(2):
        j = 128 * h
        need("v", (d_1, d_2)[h])
        k_g = done("v", V.quantize_mx(T.gq[:, j:j + 128], T.gs[:, j:j + 128], T.grb[:, 512 * h:512 * h + 512]))
        need("t", k_u, k_g)
        t_c = done("t", P.matmul_mx(T.pa[:, 1024 * h:1024 * h + 128], T.gq[:, j:j + 128], T.gs[:, j:j + 128], T.uq[:], T.us[:], True, True))
        t_f = done("t", P.matmul_mx(T.pa[:, 1024 * h + 512:1024 * h + 640], T.uq[:], T.us[:], T.gq[:, j:j + 128], T.gs[:, j:j + 128], True, True))
        need("s", t_c)
        a_c.append(done("s", S.activation(T.sth[:, h:h + 1], T.pa[:, 1024 * h:1024 * h + 1], AF.Abs, bias=TINY)))
        need("s", t_f)
        a_f.append(done("s", S.activation(T.ab[:, j:j + 128], T.pa[:, 1024 * h + 512:1024 * h + 640], AF.Abs, bias=TINY)))
        k_e = tile_e(h)

    s0, s1 = T.sth[:, 0:1], T.sth[:, 1:2]
    need("s", k_wt, a_c[1])
    a_t = done("s", S.activation(T.th[:, 128:256], T.wt[:], AF.Copy, scale=s1))
    need("v", a_c[0], k_wt)
    k_d = done("v", V.tensor_scalar(T.th[:, 0:128], T.wt[:], s0, None, A.mult))
    k_e = tile_e(2)
    need("v", a_f[0], k_d)
    done("v", V.tensor_tensor(T.cmp[:, 0:128], T.ab[:, 0:128], T.th[:, 0:128], A.is_gt))
    need("v", a_c[1])
    done("v", V.tensor_scalar(T.cmp[:, 256:384], T.ab[:, 0:128], s1, None, A.is_ge))
    need("v", a_f[1])
    k0 = done("v", V.tensor_scalar(T.cmp[:, 128:256], T.ab[:, 128:256], s0, None, A.is_gt))
    need("v", a_t)
    k1 = done("v", V.tensor_tensor(T.cmp[:, 384:512], T.ab[:, 128:256], T.th[:, 128:256], A.is_gt))
    need("v", k0)
    k0 = done("v", V.tensor_tensor_scan(T.rks[:, 0:128], T.cmp[:, 0:128], T.cmp[:, 128:256], 0.0, A.add, A.add))
    need("v", k1)
    k1 = done("v", V.tensor_tensor_scan(T.rks[:, 128:256], T.cmp[:, 256:384], T.cmp[:, 384:512], 0.0, A.add, A.add))
    rk = [T.rks[:, 127:128], T.rks[:, 255:256]]

    def ones(h):
        return done("s", S.activation(T.rst[:, 1024 * h:1024 * h + 1024], T.grb[:], AF.Copy, scale=0.0, bias=1.0))

    need("s", d_1, d_2)
    ones(0)

    need("v", k_c, k0)
    done("v", V.tensor_scalar(T.vv[:, 0:32], T.i32[:], rk[0], T.coln[:, 0:1], A.is_equal, A.mult))
    need("v", k1)
    k = done("v", V.tensor_scalar(T.vv[:, 32:64], T.i32[:], rk[1], T.coln[:, 1:2], A.is_equal, A.mult))
    need("v", k_b)
    done("v", V.tensor_scalar(T.mk[:, 0:32], T.ai[:], p4, OUT, A.not_equal, A.mult))
    need("v", k)
    for a in range(2):
        k = done("v", V.transpose(T.vt[0:64, 64 * a:64 * a + 64], T.vv[64 * a:64 * a + 64, :]))
    done("v", V.tensor_scalar(T.mk[:, 32:64], T.bi[:], p16, OUT, A.not_equal, A.mult))
    need("v", k)
    k = done("v", V.tensor_reduce(T.q4[0:64, 0:1], T.vt[0:64, :], X, A.add))
    need("v", k)
    for a in range(4):
        k = done("v", V.tensor_scalar(T.xx[32 * a:32 * a + 32, :], T.mk[0:32, :], T.q4[0:32, 0:1], T.q4[32:64, 0:1], A.add, A.add))
    need("v", k)
    k = done("v", V.transpose(T.xt[:], T.xx[:]))
    need("v", k)
    k4 = done("v", V.tensor_tensor_scan(T.sg4[:], T.r4[:], T.xt[:, 0:32], 0.0, A.mult, A.max))
    k8 = done("v", V.tensor_tensor_scan(T.sg16[:], T.r16[:], T.xt[:, 32:64], 0.0, A.mult, A.max))
    need("v", k4)
    k_o = done("v", V.tensor_scalar(T.ofo[:], T.sg4[:, 3:32:4], 4.0, p4, A.mult, A.add))
    need("v", k8)
    k_lp = done("v", V.tensor_scalar(T.lp[:, 0:2], T.sg16[:, 15:32:16], 8.0, float(rank), A.mult, A.add))
    h0 = 4 * (own0 - q0)
    need("s", k_o, d_h)
    a_h = done("s", S.activation(T.hb[:, h0 + 64:h0 + 128], T.grb[:, 0:1024].indirect(T.ofo[:, 4:8]), AF.Copy))
    need("v", k_o, d_h)
    k = done("v", V.tensor_copy(T.hb[:, h0:h0 + 64], T.grb[:, 0:1024].indirect(T.ofo[:, 0:4])))
    need("v", k, a_h)
    k_q = done("v", V.quantize_mx(T.qb[:, q0:q0 + 128], T.qs[:, q0:q0 + 128], T.hb[:]))
    a_e = done("s", S.activation(T.erb[:], T.grb[:], AF.Copy))
    mine = T.ll[:, 2 * rank:2 * rank + 2]
    need("y", k_lp)
    d_l = done("dl", Y.dma_start(mine, T.lp[:, 0:2]), 16)

    b8 = dt.uint8
    LL, C1, S1 = ("l1", n1 + len(others) * n2), ("c1", n1), ("s1", n1)
    C2, S2 = ("c2", 3 * n2), ("s2", 3 * n2)
    need("p", k_lp)
    g.remote_dma_fused([
        RemoteDMATransfer(dst_ids=ids(others), dma_engine_mask=m2, remote_sem=T.sem.l1, srcs=[T.lp[:, 0:2]], dsts=[mine for c in others]),
        RemoteDMATransfer(dst_ids=ids([partner]), dma_engine_mask=m1, remote_sem=T.sem.l1, srcs=[T.lp[:, 0:2]], dsts=[mine]),
    ], local_sem=T.sem.sent)
    need("p", k_q)
    rid, pid = topo.addr(partner, core)
    g.remote_dma(out_ap=T.qb[:, far_c:far_c + 32].bitcast(b8), in_ap=T.qb[:, own0:own0 + 32].bitcast(b8), remote_sem=T.sem.c1,
                 local_sem=T.sem.sent, pid=pid, routing_id=rid, dma_engine_mask=m1)
    hs = 0 if first else 32
    g.remote_dma_fused([RemoteDMATransfer(dst_ids=ids(helpers + [partner]), dma_engine_mask=m1, remote_sem=T.sem.s1,
                                          srcs=[T.qs[:, own0:own0 + 32]],
                                          dsts=[T.qs[:, hs:hs + 32] for h in helpers] + [T.qs[:, far_c:far_c + 32]])], local_sem=T.sem.sent)
    cnt["sent"] += 3 * n1 + n2
    need("p", C1)
    hop2(lambda i: T.cb[:, 64 * i:64 * i + 64].bitcast(b8), T.qb[:, pair0:pair0 + 64].bitcast(b8), "c2", "left")
    cnt["left"] += n2

    k_e = tile_e(3)
    f4, f8, e4, e8, x4, x8, pl, ps = [T.pf[:, 6 + i:7 + i] for i in range(8)]
    need("v", k_kk)
    done("v", V.tensor_scalar(f4, pq4, 1.0, None, A.add))
    k = done("v", V.tensor_scalar(f8, pq8, 1.0, None, A.add))
    done("v", V.tensor_scalar(e4, pq4, 3.0, 2.0, A.is_equal, A.mult))
    c = done("v", V.tensor_scalar(e8, pq8, 7.0, 2.0, A.is_equal, A.mult))
    done("v", V.tensor_scalar(pl, ph, float(BB), p1, A.mult, A.add))
    done("v", V.tensor_scalar(ps, pq8, -0.125, None, A.mult))
    need("v", k)
    done("v", V.tensor_scalar(T.ce[:, 0:32], T.k8[:], f8, HOLD, A.is_equal, A.mult))
    done("v", V.tensor_scalar(T.ce[:, 32:64], T.k4[:], f4, HOLD, A.is_equal, A.mult))
    done("v", V.tensor_scalar(T.cg[:, 0:32], T.k8[:], f8, None, A.is_gt))
    k = done("v", V.tensor_scalar(T.cg[:, 32:64], T.k4[:], f4, None, A.is_gt))
    need("v", c)
    done("v", V.tensor_scalar(x4, e4, 2.0 / HOLD, None, A.max))
    done("v", V.tensor_scalar(x8, e8, 2.0 / HOLD, None, A.max))
    need("v", k)
    done("v", V.tensor_tensor(T.ch8[:, 0:32], T.ce[:, 0:32], T.cg[:, 0:32], A.max))
    a_ch = done("v", V.tensor_tensor(T.ch4[:, 0:32], T.ce[:, 32:64], T.cg[:, 32:64], A.max))

    def decode(ps, n, codes, scales):
        return [done("t", P.matmul_mx(ps[:, 512 * b:512 * b + n], T.eq[:, 128 * b:128 * b + 128], T.es[:, 128 * b:128 * b + 128],
                                      codes, scales, True, True)) for b in range(4)]

    def empty(q, tok, dst, src):
        need(q, tok)
        if q == "s":
            return done("s", S.activation(dst, src, AF.Copy))
        return done("v", V.tensor_copy(dst, src))

    need("t", k_e, a_f[1], k_q)
    td = decode(T.pa, 128, T.qb[:, q0:q0 + 128], T.qs[:, q0:q0 + 128])
    vo = [empty("s" if b % 2 else "v", td[b], T.vo[:, b:128:4], T.pa[:, 512 * b + own0 - q0:512 * b + own0 - q0 + 32]) for b in range(4)]
    need("s", k1)
    for h in range(2):
        a_rk = done("s", S.activation(T.rkf[:, h:h + 1], rk[h], AF.Copy))
    a_r = ones(1)
    need("v", a_e, *vo)
    k = done("v", V.tensor_tensor(T.te[:], T.erb[:, 0:1024].indirect(T.ofo[:, 0:8]), T.vo[:], A.subtract))
    need("v", a_rk)
    done("v", V.tensor_scalar(T.wv[:, 0:32], T.i32[:], T.rkf[:, 0:1], T.sth[:, 0:1], A.is_equal, A.mult))
    w = done("v", V.tensor_scalar(T.wv[:, 32:64], T.i32[:], T.rkf[:, 1:2], T.sth[:, 1:2], A.is_equal, A.mult))
    need("v", k)
    k_er = done("v", V.tensor_copy(T.erb[:, 0:1024].indirect(T.ofo[:, 0:8]), T.te[:]))
    need("y", k_er, ("left", n2))
    d_er = done("der", Y.dma_start(T.er[:], T.erb[:]), 16)
    need("v", w)
    for a in range(2):
        w = done("v", V.transpose(T.wt2[0:64, 64 * a:64 * a + 64], T.wv[64 * a:64 * a + 64, :]))
    need("v", a_r)
    k_r = done("v", V.memset(T.rst[:, 0:2048:8], 0.0))
    need("v", w)
    w = done("v", V.tensor_reduce(T.wq[0:64, 0:1], T.wt2[0:64, :], X, A.add))
    need("v", w)
    w = done("v", V.tensor_scalar(T.wx[0:32, 0:1], T.wq[0:32, 0:1], T.wq[32:64, 0:1], TINY, A.add, A.subtract))
    need("v", w)
    w = done("v", V.transpose(T.wy[0:32, :], T.wx[0:32, :]))
    need("y", w)
    d_sc = done("dsc", Y.dma_start(T.sc[:], T.wy[0:1, :]), 16)
    for n in (32, 64, 128):
        need("s", a_ch)
        done("s", S.activation(T.ch8[:, n:2 * n], T.ch8[:, 0:n], AF.Copy))
        a_ch = done("s", S.activation(T.ch4[:, n:2 * n], T.ch4[:, 0:n], AF.Copy))

    need("t", C1, S1, *vo)
    td = decode(T.pa, 128, T.qb[:, dec0:dec0 + 128], T.qs[:, dec0:dec0 + 128])
    for b in range(4):
        h, i, c0 = b // 2, b % 2, 512 * b + pair0 - dec0
        if me == 0:
            empty("s", td[b], T.tv[:, BB * h + 2 + i:BB * h + 66:2], T.pa[:, c0:c0 + 32])
            a_p = empty("s", td[b], T.vb[:, 512 * h + 64 + i:512 * h + 128:2], T.pa[:, c0 + 32:c0 + 64])
        else:
            a_p = empty("s", td[b], T.vb[:, 512 * h + i:512 * h + 128:2], T.pa[:, c0:c0 + 64])

    need("v", LL, d_l, a_en, d_m, a_ch, k_r)
    k = done("v", V.tensor_copy(T.m8[:, 0:2048].indirect(T.ll[:, 0:16]), T.ent[:]))
    n = done("v", V.tensor_copy(T.lf[0:32, 0:16], T.ll[0:32, 0:16]))
    need("v", k)
    k = done("v", V.tensor_tensor_scan(T.mp[:, 1:2049], T.rst[:], T.m8[:], 0.0, A.mult, A.max))
    need("v", n)
    n = done("v", V.transpose(T.nt[0:32, :], T.lf[0:32, :]))
    need("v", k)
    k = done("v", V.tensor_copy(T.pr[:, 0:224], T.mp[:, 0:2048].indirect(T.ll[:, 2:16])))
    need("v", n)
    k_nb = done("v", V.tensor_scalar(T.nu[0:32, :], T.nt[0:32, :], 0.125, T.pf[0:32, 13:14], A.mult, A.add))
    need("v", k)
    k = done("v", V.tensor_tensor_scan(T.hp[:, 0:224], T.ch8[:, 0:224], T.pr[:, 0:224], 0.0, A.mult, A.add))
    need("v", k)
    k_op = done("v", V.tensor_scalar(T.offp[:, 0:28], T.hp[:, 7:224:8], x8, p1, A.mult, A.add))
    need("y", k_nb)
    d_nb = done("dnb", Y.dma_start(T.nb[:], T.nu[0:16, 0:16]), 16)

    need("t", C2, S2)
    td = decode(T.pb, 192, T.cb[:], T.cs[:])
    got = [[], []]

    def landed(b, part):
        h, i, q, n = b // 2, b % 2, "s" if b % 2 else "v", 0 if me == 0 else 32
        if part == 0 and n:
            got[h].append(empty(q, td[b], T.tv[:, BB * h + 2 + i:BB * h + 66:2], T.pb[:, 512 * b:512 * b + 32]))
        if part == 1:
            got[h].append(empty(q, td[b], T.vb[:, 512 * h + 128 + 2 * n + i:512 * h + 512:2], T.pb[:, 512 * b + n:512 * b + 192]))

    for b in (0, 1, 3):
        landed(b, 0)
        landed(b, 1)

    last = [None, None]

    def add(h, s):
        m = s // 2
        at = (s % 2) if m == me else 2 + 2 * slot(m, me) + s % 2
        need("v", k_op, a_p, *got[h])
        if last[h]:
            need("v", last[h])
        last[h] = done("v", V.tensor_tensor(T.tv[:, BB * h + 2 + 64 * s:BB * h + 66 + 64 * s],
                                            T.tv[:, BB * h:BB * h + 2 + 64 * s].indirect(T.offp[:, 4 * s - 4:4 * s]),
                                            T.vb[:, 512 * h + 64 * at:512 * h + 64 * at + 64], A.add))

    for s in range(1, 10):
        if s < 8:
            add(0, s)
        if s < 3:
            landed(2, s - 1)
        else:
            add(1, s - 2)
        if s == 7:
            k_hl = done("v", V.tensor_tensor_scan(T.hl[:], T.ch4[:], T.mp[:, 8:2049:8], 0.0, A.mult, A.add))
        if s == 8:
            need("v", k_hl)
            k_ol = done("v", V.tensor_scalar(T.offl[:], T.hl[:, 3:256:4], x4, pl, A.mult, A.add))

    need("v", k_ol, *last)
    need("s", k_ol, *last)
    win, parts = T.tv[:, 0:BB + 514], []
    for i in range(2):
        parts.append((256 * i, done("v", V.tensor_copy(T.acb[:, 256 * i:256 * i + 256], win.indirect(T.offl[:, 16 * i:16 * i + 16])))))
        parts.append((512 + 256 * i, done("s", S.activation(T.acb[:, 512 + 256 * i:768 + 256 * i], win.indirect(T.offl[:, 32 + 16 * i:48 + 16 * i]), AF.Copy))))
    for c, tok in parts:
        q = "s" if tok == parts[-1][1] else "y"
        need(q, tok)
        d_ac = done("dac", Q[q].dma_start(T.acc[:, c:c + 256], T.acb[:, c:c + 256]), 16)

    need("p", d_u, d_1, d_2, d_h, d_m, d_l, d_er, d_nb, d_ac, d_sc, LL, C2, S2)
    need("p", *[(x, cnt[x]) for x in ("v", "s", "t", "p", "sent", "left")])
